import numpy as np
import ml_dtypes


def mxq(x, axis, fmt="e4m3"):
    dtype, down = {"e4m3": (ml_dtypes.float8_e4m3fn, 7), "e5m2": (ml_dtypes.float8_e5m2, 14)}[fmt]
    v = np.moveaxis(np.asarray(x, np.float32).astype(ml_dtypes.bfloat16).astype(np.float64), axis, -1)
    blocks = v.reshape(v.shape[:-1] + (-1, 32))
    amax = np.abs(blocks).max(-1, keepdims=True)
    byte = np.maximum(np.where(amax > 0, np.frexp(amax)[1] - 1 + 127, 0) - down, 1)
    scale = np.exp2(byte - 127.0)
    codes = (blocks / scale).astype(np.float32).astype(dtype).astype(np.float64)
    return np.moveaxis((codes * scale).reshape(v.shape), -1, axis)


WIDE = False


def mx_kscale(k):
    if not WIDE:
        return np.ones(k)
    levels = np.array([10, -10, 5, -5, 0])
    if k % 512:
        return np.exp2(np.random.permutation(np.resize(levels, k // 32))).repeat(32)
    a = np.empty((k // 512, 16))
    for p in range(k // 512):
        a[p, :8] = np.random.permutation(np.resize(levels, 8))
        for g in range(8):
            far = levels[np.abs(levels - a[p, g]) >= 10]
            a[p, g + 8] = far[np.random.randint(len(far))]
    return np.exp2(a.ravel()).repeat(32)


def f64(x):
    return np.asarray(x).astype(np.float64)


def striped(idx):
    return np.tile(idx.reshape(-1, 16).T, (8, 1)).astype(np.uint16)


def unstriped(offs):
    return offs[:16].T.reshape(-1).astype(np.int64)


E2M1 = np.array([0.0, 0.5, 1.0, 1.5, 2.0, 3.0, 4.0, 6.0, -0.0, -0.5, -1.0, -1.5, -2.0, -3.0, -4.0, -6.0])


def pack_weight(w, fmt):
    k, n = w.shape
    w = f64(np.asarray(w, np.float32).astype(ml_dtypes.bfloat16)).reshape(k // 32, 32, n)
    amax = np.abs(w).max(1)
    if fmt == "e4m3":
        byte = np.frexp(amax)[1] - 1 + 127 - 7
    else:
        mant, ex = np.frexp(amax / 6.0)
        byte = np.where(mant > 0.5, ex, ex - 1) + 127
    byte = np.clip(np.where(amax > 0, byte, 1), 1, 254)
    scaled = (w * np.exp2(127.0 - byte)[:, None, :]).reshape(k, n).astype(np.float32)
    by_word = np.ascontiguousarray(scaled.reshape(k // 512, 128, 4, n).transpose(0, 1, 3, 2))
    if fmt == "e4m3":
        words = by_word.astype(ml_dtypes.float8_e4m3fn).view(np.uint8)
    else:
        c = by_word.astype(ml_dtypes.float4_e2m1fn).view(np.uint8) & 0xF
        words = (c[..., 0::2] | (c[..., 1::2] << 4)).reshape(k // 512, 128, 2 * n)
    return np.ascontiguousarray(words), np.ascontiguousarray(byte.astype(np.uint8).reshape(k // 512, 16, n))


def unpack_weight(words, scales, fmt):
    g, _, n = scales.shape
    words = np.ascontiguousarray(words).reshape(g, 128, n, -1)
    if fmt == "e4m3":
        vals = words.view(ml_dtypes.float8_e4m3fn).astype(np.float64)
    else:
        nib = np.empty((g, 128, n, 4), np.uint8)
        nib[..., 0::2] = words & 0xF
        nib[..., 1::2] = words >> 4
        vals = E2M1[nib]
    vals = vals * np.repeat(np.exp2(scales.astype(np.float64) - 127.0), 8, axis=1)[..., None]
    return vals.transpose(0, 1, 3, 2).reshape(g * 512, n)


def gelu(v):
    return 0.5 * v * (1.0 + np.tanh(np.sqrt(2.0 / np.pi) * (v + 0.044715 * v**3)))


K, N, T, S, M = 1024, 1024, 2048, 512, 1024

def setup_inputs():
    n = np.random.standard_normal
    s = mx_kscale(K)[:, None]
    u = mx_kscale(S)
    idx = np.random.permutation(T)[:S]
    tab_words, tab_scales = pack_weight(n((K, T)) * s / np.sqrt(K), "e4m3")
    w4_words, w4_scales = pack_weight(n((K, N)) * s / np.sqrt(K), "e2m1")
    wdT = n((N, T)) / np.sqrt(S)
    wdT[:, idx] /= u
    return {
        "x": (n((K, M)) / s).astype(np.float32),
        "x0": n((N, M)).astype(np.float32),
        "tab_words": tab_words, "tab_scales": tab_scales,
        "offs": striped(idx),
        "g": (np.exp(0.3 * n(S)) * u).astype(np.float32),
        "wdT": wdT.astype(np.float32),
        "w4_words": w4_words, "w4_scales": w4_scales,
        "b": (0.5 * n(N)).astype(np.float32),
        "a": (np.exp(0.3 * n(N)) * s[:, 0]).astype(np.float32),
    }

def reference(x, x0, tab_words, tab_scales, offs, g, wdT, w4_words, w4_scales, b, a):
    v = unpack_weight(tab_words, tab_scales, "e4m3")[:, unstriped(offs)]
    w4 = unpack_weight(w4_words, w4_scales, "e2m1")
    wd = f64(wdT)[:, unstriped(offs)]
    xq = mxq(f64(x), 0, "e4m3")
    h = f64(g)[:, None] * (v.T @ xq)
    y = w4.T @ xq + mxq(wd, 1, "e4m3") @ mxq(h, 0, "e4m3")
    return f64(x0) * (y + f64(b)[:, None]) + f64(a)[:, None] * f64(x)

@@ -1,0 +1,229 @@
+from contextlib import ExitStack
+
+import concourse.mybir as mybir
+from concourse.masks import make_identity
+
+K, N, T, S, M = 1024, 1024, 2048, 512, 1024
+FLOPS = 2 * M * (K * S + K * N + S * N)
+
+F32 = mybir.dt.float32
+BF16 = mybir.dt.bfloat16
+I32 = mybir.dt.int32
+U32 = mybir.dt.uint32
+U16 = mybir.dt.uint16
+U8 = mybir.dt.uint8
+FP8X4 = mybir.dt.float8_e4m3fn_x4
+FP4X4 = mybir.dt.float4_e2m1fn_x4
+MULT = mybir.AluOpType.mult
+ADD = mybir.AluOpType.add
+COPY = mybir.ActivationFunctionType.Copy
+
+P = 128
+PACK = 4
+K_PASS = P * PACK
+PASSES = K // K_PASS
+HALF = 512
+HALVES = M // HALF
+N_TILES = N // P
+
+
+def tile_list_lowrank_cross_layer_kernel(
+    tc, x, x0, tab_words, tab_scales, offs, g, wdT, w4_words, w4_scales, b, a, out
+):
+    nc = tc.nc
+    with ExitStack() as ctx:
+        keep = ctx.enter_context(tc.tile_pool(name="keep", bufs=1))
+        ring = ctx.enter_context(tc.tile_pool(name="ring", bufs=2))
+        h_banks = ctx.enter_context(tc.psum_pool(name="h_banks", bufs=2))
+        t_banks = ctx.enter_context(tc.psum_pool(name="t_banks", bufs=2))
+        y_banks = ctx.enter_context(tc.psum_pool(name="y_banks", bufs=4))
+
+        offsets = keep.tile([P, S // 16], U16, name="offsets")
+        w4_raw = keep.tile([P, PASSES, 2 * N], U8, name="w4_raw", align_bytes=64)
+        w4s_raw = keep.tile([P, PASSES, N], U8, name="w4s_raw", align_bytes=64)
+        tabs_raw = keep.tile([P, T], U8, name="tabs_raw", align_bytes=64)
+        tab_raw = [keep.tile([P, T], I32, name="tab_raw%d" % c, align_bytes=64) for c in range(PASSES)]
+        x_raw = [keep.tile([P, HALVES, PACK, HALF], F32, name="x_raw%d" % c) for c in range(PASSES)]
+        wd_raw = [keep.tile([P, T], F32, name="wd_raw%d" % i) for i in range(N_TILES)]
+        x0_sb = [keep.tile([P, M], F32, name="x0_sb%d" % i) for i in range(N_TILES)]
+        g_sb = keep.tile([P, PACK], F32, name="g_sb")
+        a_sb = keep.tile([P, PASSES, PACK], F32, name="a_sb")
+        b_sb = keep.tile([P, PASSES, PACK], F32, name="b_sb")
+        ident = keep.tile([P, P], F32, name="ident")
+
+        nc.vector.memset(w4s_raw[:].rearrange("p c n -> p (c n)").bitcast(I32), 0)
+        nc.gpsimd.memset(tabs_raw[:].bitcast(I32), 0)
+        make_identity(nc, ident[:])
+
+        x_rows = x.rearrange("(c p t) m -> c p t m", p=P, t=PACK)
+        x0_rows = x0.rearrange("(c p t) m -> c p t m", p=P, t=PACK)
+        out_rows = out.rearrange("(c p t) m -> c p t m", p=P, t=PACK)
+        wd_rows = wdT.rearrange("(c p t) j -> c t p j", p=P, t=PACK)
+
+        def load_x(c, hf):
+            nc.sync.dma_start(out=x_raw[c][:, hf], in_=x_rows[c][:, :, hf * HALF:(hf + 1) * HALF])
+
+        def load_wd(i):
+            nc.sync.dma_start(out=wd_raw[i][:], in_=wd_rows[i // PACK][i % PACK])
+
+        def load_x0(i):
+            nc.sync.dma_start(out=x0_sb[i][:], in_=x0_rows[i // PACK][:, i % PACK, :])
+
+        nc.sync.dma_start(offsets[:], offs)
+        nc.sync.dma_start(out=w4_raw[:].bitcast(I32), in_=w4_words.rearrange("c p n -> p c n").bitcast(I32))
+        for q in range(4):
+            nc.sync.dma_start(out=w4s_raw[32 * q:32 * q + 4].bitcast(I32),
+                              in_=w4_scales[:, 4 * q:4 * q + 4, :].rearrange("c r n -> r c n").bitcast(I32))
+        nc.sync.dma_start(out=tab_raw[0][:], in_=tab_words[0].rearrange("p n t -> p (n t)").bitcast(I32))
+        for q in range(4):
+            nc.sync.dma_start(out=tabs_raw[32 * q:32 * q + 8, :].bitcast(I32),
+                              in_=tab_scales[:, 4 * q:4 * q + 4, :].bitcast(I32))
+        nc.sync.dma_start(out=tab_raw[1][:], in_=tab_words[1].rearrange("p n t -> p (n t)").bitcast(I32))
+        load_x(0, 0)
+        load_x(1, 0)
+        nc.sync.dma_start(out=g_sb[:], in_=g.rearrange("(p t) -> p t", t=PACK))
+        load_x(0, 1)
+        load_x(1, 1)
+        nc.sync.dma_start(out=a_sb[:], in_=a.rearrange("(c p t) -> p c t", p=P, t=PACK))
+        nc.sync.dma_start(out=b_sb[:], in_=b.rearrange("(c p t) -> p c t", p=P, t=PACK))
+        load_wd(0)
+        for i in range(N_TILES):
+            if i + 1 < N_TILES:
+                load_wd(i + 1)
+            load_x0(i)
+
+        w4q = keep.tile([P, PASSES, 2 * N], U8, name="w4q", align_bytes=64)
+        w4s = keep.tile([P, PASSES, N], U8, name="w4s", align_bytes=64)
+        nc.vector.tensor_copy(
+            out=w4q[:].rearrange("p c n -> p (c n)").bitcast(U16).rearrange("p (c t q) -> p c t q", t=PACK, q=P),
+            in_=w4_raw[:].rearrange("p c n -> p (c n)").bitcast(U16).rearrange("p (c q t) -> p c t q", t=PACK, q=P))
+        nc.vector.tensor_copy(
+            out=w4s[:].rearrange("p c (d t q) -> p (c d) t q", t=PACK, q=P),
+            in_=w4s_raw[:].rearrange("p c (d q t) -> p (c d) t q", t=PACK, q=P))
+
+        vq = [keep.tile([P, S], U32, name="vq%d" % c, align_bytes=64) for c in range(PASSES)]
+        vs_listed = keep.tile([P, S], U8, name="vs_listed", align_bytes=64)
+        vs = keep.tile([P, S], U8, name="vs", align_bytes=64)
+        nc.vector.tensor_copy(out=vq[0][:].rearrange("p (t q) -> p q t", t=PACK),
+                              in_=tab_raw[0][:].bitcast(U32).indirect(offsets[:]))
+        nc.vector.tensor_copy(out=vs_listed[:], in_=tabs_raw[:].indirect(offsets[:]))
+        nc.vector.tensor_copy(out=vq[1][:].rearrange("p (t q) -> p q t", t=PACK),
+                              in_=tab_raw[1][:].bitcast(U32).indirect(offsets[:]))
+        nc.vector.tensor_copy(out=vs[:].rearrange("p (t q) -> p t q", t=PACK),
+                              in_=vs_listed[:].rearrange("p (q t) -> p t q", t=PACK))
+
+        xq = {}
+        xs = {}
+
+        for c in range(PASSES):
+            for hf in range(HALVES):
+                xq[c, hf] = keep.tile([P, HALF], U32, name="xq%d%d" % (c, hf), align_bytes=64)
+                xs[c, hf] = keep.tile([P, HALF], U8, name="xs%d%d" % (c, hf), align_bytes=64)
+
+        def weave_x(copy, c, hf, cols):
+            woven = ring.tile([P, cols.stop - cols.start, PACK], BF16, name="x_woven", align_bytes=64, bufs=4)
+            copy(out=woven[:].rearrange("p (m i) t -> p m t i", i=4),
+                 in_=x_raw[c][:, hf, :, cols].rearrange("p t (m i) -> p m t i", i=4))
+            return woven
+
+        def quantise_x(woven, c, hf, cols):
+            nc.vector.quantize_mx(out=xq[c, hf][:, cols].bitcast(FP8X4), scales=xs[c, hf][:, cols],
+                                  in_=woven[:].rearrange("p m t -> p (m t)"))
+
+        def prepare_x(hf):
+            whole, low, high = slice(0, HALF), slice(0, HALF // 2), slice(HALF // 2, HALF)
+            quantise_x(weave_x(nc.scalar.copy, 0, hf, whole), 0, hf, whole)
+            first = weave_x(nc.vector.tensor_copy, 1, hf, low)
+            second = weave_x(nc.scalar.copy, 1, hf, high)
+            quantise_x(first, 1, hf, low)
+            quantise_x(second, 1, hf, high)
+
+        hq = [keep.tile([P, HALF], U32, name="hq%d" % hf, align_bytes=64) for hf in range(HALVES)]
+        hs = [keep.tile([P, HALF], U8, name="hs%d" % hf, align_bytes=64) for hf in range(HALVES)]
+
+        def h_pass(dst, t, c, hf, cols):
+            nc.tensor.matmul_mx(out=dst, lhsT=vq[c][:, t * P:(t + 1) * P].bitcast(FP8X4),
+                                lhsT_scale=vs[4 * c:, t * P:(t + 1) * P],
+                                rhs=xq[c, hf][:, cols].bitcast(FP8X4), rhs_scale=xs[c, hf][:, cols],
+                                start=(c == 0), stop=(c == PASSES - 1))
+
+        def h_on_vector(hf):
+            woven = []
+            for mb in range(HALF // P):
+                cols = slice(mb * P, (mb + 1) * P)
+                bank = h_banks.tile([P, PACK, P], F32, name="h_bank")
+                for t in range(PACK):
+                    for c in range(PASSES):
+                        h_pass(bank[:, t, :], t, c, hf, cols)
+                woven.append(ring.tile([P, P, PACK], BF16, name="h_woven", align_bytes=64))
+                nc.vector.tensor_tensor(out=woven[mb][:], in0=bank[:].rearrange("p t m -> p m t"),
+                                        in1=g_sb[:].unsqueeze(1).to_broadcast([P, P, PACK]), op=MULT)
+                if mb > 0:
+                    quantise_h(hf, mb - 1, woven[mb - 1])
+            quantise_h(hf, HALF // P - 1, woven[-1])
+
+        def quantise_h(hf, mb, woven):
+            cols = slice(mb * P, (mb + 1) * P)
+            nc.vector.quantize_mx(out=hq[hf][:, cols].bitcast(FP8X4), scales=hs[hf][:, cols],
+                                  in_=woven[:].rearrange("p m t -> p (m t)"))
+
+        wdq = [keep.tile([P, P], U32, name="wdq%d" % i, align_bytes=64) for i in range(N_TILES)]
+        wds = [keep.tile([P, P], U8, name="wds%d" % i, align_bytes=64) for i in range(N_TILES)]
+        wd_woven = {}
+
+        def gather_wd(i):
+            listed = ring.tile([P, S], BF16, name="wd_listed", align_bytes=64)
+            nc.vector.tensor_copy(out=listed[:], in_=wd_raw[i][:].indirect(offsets[:]))
+            pairs = listed[:].bitcast(F32)
+            bank = t_banks.tile([P, 2, P], F32, name="t_bank")
+            for u in range(2):
+                nc.tensor.transpose(bank[:, u, :], pairs[:, u:S // 2:2], ident[:])
+            wd_woven[i] = ring.tile([P, P * PACK], BF16, name="wd_woven", align_bytes=64)
+            nc.scalar.copy(out=wd_woven[i][:].bitcast(F32).rearrange("p (n u) -> p n u", u=2),
+                           in_=bank[:].rearrange("p u n -> p n u"))
+
+        def quantise_wd(i):
+            nc.vector.quantize_mx(out=wdq[i][:].bitcast(FP8X4), scales=wds[i][:], in_=wd_woven[i][:])
+
+        def cross(i, hf):
+            c_out, t = i // PACK, i % PACK
+            bank = y_banks.tile([P, HALF], F32, name="y_bank")
+            for c in range(PASSES):
+                nc.tensor.matmul_mx(out=bank[:], lhsT=w4q[:, c, 2 * i * P:2 * (i + 1) * P].bitcast(FP4X4),
+                                    lhsT_scale=w4s[:, c, i * P:(i + 1) * P],
+                                    rhs=xq[c, hf][:].bitcast(FP8X4), rhs_scale=xs[c, hf][:],
+                                    start=(c == 0), stop=False)
+            nc.tensor.matmul_mx(out=bank[:], lhsT=wdq[i][:].bitcast(FP8X4), lhsT_scale=wds[i][:],
+                                rhs=hq[hf][:].bitcast(FP8X4), rhs_scale=hs[hf][:], start=False, stop=True)
+            dst = x0_sb[i][:, hf * HALF:(hf + 1) * HALF]
+            nc.vector.scalar_tensor_tensor(out=dst, in0=bank[:], scalar=b_sb[:, c_out, t:t + 1], in1=dst,
+                                           op0=ADD, op1=MULT)
+
+        def add_skip(i, hf):
+            c_out, t = i // PACK, i % PACK
+            dst = x0_sb[i][:, hf * HALF:(hf + 1) * HALF]
+            nc.vector.scalar_tensor_tensor(out=dst, in0=x_raw[c_out][:, hf, t, :], scalar=a_sb[:, c_out, t:t + 1],
+                                           in1=dst, op0=MULT, op1=ADD)
+
+        def store(i, cols):
+            nc.sync.dma_start(out=out_rows[i // PACK][:, i % PACK, cols], in_=x0_sb[i][:, cols])
+
+        prepare_x(0)
+        h_on_vector(0)
+        prepare_x(1)
+        h_on_vector(1)
+        gather_wd(0)
+        quantise_wd(0)
+        for i in range(N_TILES):
+            last = i + 1 == N_TILES
+            if not last:
+                gather_wd(i + 1)
+            for hf in range(HALVES):
+                cross(i, hf)
+            for hf in range(HALVES):
+                add_skip(i, hf)
+                if last:
+                    store(i, slice(hf * HALF, (hf + 1) * HALF))
+            if not last:
+                store(i, slice(0, M))
+                quantise_wd(i + 1)

@@ -25,6 +25,10 @@ PASSES = K // K_PASS
 HALF = 512
 HALVES = M // HALF
 N_TILES = N // P
+WD_AHEAD = 2
+RUN = 4
+QUADRANTS = (0, 2, 1, 3)
+STORES = ((0, 4), (4, 2), (6, 1))
 
 
 def tile_list_lowrank_cross_layer_kernel(
@@ -34,21 +38,22 @@ def tile_list_lowrank_cross_layer_kernel(
     with ExitStack() as ctx:
         keep = ctx.enter_context(tc.tile_pool(name="keep", bufs=1))
         ring = ctx.enter_context(tc.tile_pool(name="ring", bufs=2))
-        h_banks = ctx.enter_context(tc.psum_pool(name="h_banks", bufs=2))
-        t_banks = ctx.enter_context(tc.psum_pool(name="t_banks", bufs=2))
+        h_banks = ctx.enter_context(tc.psum_pool(name="h_banks", bufs=3))
+        t_banks = ctx.enter_context(tc.psum_pool(name="t_banks", bufs=1))
         y_banks = ctx.enter_context(tc.psum_pool(name="y_banks", bufs=4))
 
         offsets = keep.tile([P, S // 16], U16, name="offsets")
-        w4_raw = keep.tile([P, PASSES, 2 * N], U8, name="w4_raw", align_bytes=64)
+        w4_raw = [keep.tile([P, 2 * N], U8, name="w4_raw%d" % c, align_bytes=64) for c in range(PASSES)]
         w4s_raw = keep.tile([P, PASSES, N], U8, name="w4s_raw", align_bytes=64)
         tabs_raw = keep.tile([P, T], U8, name="tabs_raw", align_bytes=64)
         tab_raw = [keep.tile([P, T], I32, name="tab_raw%d" % c, align_bytes=64) for c in range(PASSES)]
         x_raw = [keep.tile([P, HALVES, PACK, HALF], F32, name="x_raw%d" % c) for c in range(PASSES)]
         wd_raw = [keep.tile([P, T], F32, name="wd_raw%d" % i) for i in range(N_TILES)]
-        x0_sb = [keep.tile([P, M], F32, name="x0_sb%d" % i) for i in range(N_TILES)]
+        x0_pass = [keep.tile([P, PACK, M], F32, name="x0_pass%d" % c) for c in range(PASSES)]
+        x0_sb = [x0_pass[i // PACK][:, i % PACK, :] for i in range(N_TILES)]
         g_sb = keep.tile([P, PACK], F32, name="g_sb")
-        a_sb = keep.tile([P, PASSES, PACK], F32, name="a_sb")
-        b_sb = keep.tile([P, PASSES, PACK], F32, name="b_sb")
+        a_sb = [keep.tile([P, PACK], F32, name="a_sb%d" % c) for c in range(PASSES)]
+        b_sb = [keep.tile([P, PACK], F32, name="b_sb%d" % c) for c in range(PASSES)]
         ident = keep.tile([P, P], F32, name="ident")
 
         nc.vector.memset(w4s_raw[:].rearrange("p c n -> p (c n)").bitcast(I32), 0)
@@ -67,36 +72,39 @@ def tile_list_lowrank_cross_layer_kernel(
             nc.sync.dma_start(out=wd_raw[i][:], in_=wd_rows[i // PACK][i % PACK])
 
         def load_x0(i):
-            nc.sync.dma_start(out=x0_sb[i][:], in_=x0_rows[i // PACK][:, i % PACK, :])
+            nc.sync.dma_start(out=x0_sb[i], in_=x0_rows[i // PACK][:, i % PACK, :])
 
         nc.sync.dma_start(offsets[:], offs)
-        nc.sync.dma_start(out=w4_raw[:].bitcast(I32), in_=w4_words.rearrange("c p n -> p c n").bitcast(I32))
-        for q in range(4):
+        nc.sync.dma_start(out=g_sb[:], in_=g.rearrange("(p t) -> p t", t=PACK))
+        for c in range(PASSES):
+            nc.sync.dma_start(out=a_sb[c][:], in_=a.rearrange("(c p t) -> c p t", p=P, t=PACK)[c])
+            nc.sync.dma_start(out=b_sb[c][:], in_=b.rearrange("(c p t) -> c p t", p=P, t=PACK)[c])
+        for c in range(PASSES):
+            nc.sync.dma_start(out=w4_raw[c][:].bitcast(I32), in_=w4_words[c].bitcast(I32))
+        for q in QUADRANTS:
             nc.sync.dma_start(out=w4s_raw[32 * q:32 * q + 4].bitcast(I32),
                               in_=w4_scales[:, 4 * q:4 * q + 4, :].rearrange("c r n -> r c n").bitcast(I32))
         nc.sync.dma_start(out=tab_raw[0][:], in_=tab_words[0].rearrange("p n t -> p (n t)").bitcast(I32))
-        for q in range(4):
+        for q in QUADRANTS:
             nc.sync.dma_start(out=tabs_raw[32 * q:32 * q + 8, :].bitcast(I32),
                               in_=tab_scales[:, 4 * q:4 * q + 4, :].bitcast(I32))
         nc.sync.dma_start(out=tab_raw[1][:], in_=tab_words[1].rearrange("p n t -> p (n t)").bitcast(I32))
-        load_x(0, 0)
-        load_x(1, 0)
-        nc.sync.dma_start(out=g_sb[:], in_=g.rearrange("(p t) -> p t", t=PACK))
-        load_x(0, 1)
-        load_x(1, 1)
-        nc.sync.dma_start(out=a_sb[:], in_=a.rearrange("(c p t) -> p c t", p=P, t=PACK))
-        nc.sync.dma_start(out=b_sb[:], in_=b.rearrange("(c p t) -> p c t", p=P, t=PACK))
-        load_wd(0)
+        for hf in range(HALVES):
+            for c in range(PASSES):
+                load_x(c, hf)
+        for i in range(WD_AHEAD):
+            load_wd(i)
         for i in range(N_TILES):
-            if i + 1 < N_TILES:
-                load_wd(i + 1)
+            if i + WD_AHEAD < N_TILES:
+                load_wd(i + WD_AHEAD)
             load_x0(i)
 
         w4q = keep.tile([P, PASSES, 2 * N], U8, name="w4q", align_bytes=64)
         w4s = keep.tile([P, PASSES, N], U8, name="w4s", align_bytes=64)
-        nc.vector.tensor_copy(
-            out=w4q[:].rearrange("p c n -> p (c n)").bitcast(U16).rearrange("p (c t q) -> p c t q", t=PACK, q=P),
-            in_=w4_raw[:].rearrange("p c n -> p (c n)").bitcast(U16).rearrange("p (c q t) -> p c t q", t=PACK, q=P))
+        for c in range(PASSES):
+            nc.vector.tensor_copy(
+                out=w4q[:, c, :].bitcast(U16).rearrange("p (d t q) -> p d t q", t=PACK, q=P),
+                in_=w4_raw[c][:].bitcast(U16).rearrange("p (d q t) -> p d t q", t=PACK, q=P))
         nc.vector.tensor_copy(
             out=w4s[:].rearrange("p c (d t q) -> p (c d) t q", t=PACK, q=P),
             in_=w4s_raw[:].rearrange("p c (d q t) -> p (c d) t q", t=PACK, q=P))
@@ -114,29 +122,28 @@ def tile_list_lowrank_cross_layer_kernel(
 
         xq = {}
         xs = {}
-
         for c in range(PASSES):
             for hf in range(HALVES):
                 xq[c, hf] = keep.tile([P, HALF], U32, name="xq%d%d" % (c, hf), align_bytes=64)
                 xs[c, hf] = keep.tile([P, HALF], U8, name="xs%d%d" % (c, hf), align_bytes=64)
 
         def weave_x(copy, c, hf, cols):
-            woven = ring.tile([P, cols.stop - cols.start, PACK], BF16, name="x_woven", align_bytes=64, bufs=4)
-            copy(out=woven[:].rearrange("p (m i) t -> p m t i", i=4),
-                 in_=x_raw[c][:, hf, :, cols].rearrange("p t (m i) -> p m t i", i=4))
+            woven = ring.tile([P, cols.stop - cols.start, PACK], BF16, name="x_woven", align_bytes=64, bufs=6)
+            copy(out=woven[:].rearrange("p (m i) t -> p m t i", i=RUN),
+                 in_=x_raw[c][:, hf, :, cols].rearrange("p t (m i) -> p m t i", i=RUN))
             return woven
 
         def quantise_x(woven, c, hf, cols):
             nc.vector.quantize_mx(out=xq[c, hf][:, cols].bitcast(FP8X4), scales=xs[c, hf][:, cols],
                                   in_=woven[:].rearrange("p m t -> p (m t)"))
 
-        def prepare_x(hf):
-            whole, low, high = slice(0, HALF), slice(0, HALF // 2), slice(HALF // 2, HALF)
-            quantise_x(weave_x(nc.scalar.copy, 0, hf, whole), 0, hf, whole)
-            first = weave_x(nc.vector.tensor_copy, 1, hf, low)
-            second = weave_x(nc.scalar.copy, 1, hf, high)
-            quantise_x(first, 1, hf, low)
-            quantise_x(second, 1, hf, high)
+        low, high = slice(0, HALF // 2), slice(HALF // 2, HALF)
+
+        def prepare_x(c, hf, copy_low, copy_high):
+            first = weave_x(copy_low, c, hf, low)
+            second = weave_x(copy_high, c, hf, high)
+            quantise_x(first, c, hf, low)
+            quantise_x(second, c, hf, high)
 
         hq = [keep.tile([P, HALF], U32, name="hq%d" % hf, align_bytes=64) for hf in range(HALVES)]
         hs = [keep.tile([P, HALF], U8, name="hs%d" % hf, align_bytes=64) for hf in range(HALVES)]
@@ -147,7 +154,12 @@ def tile_list_lowrank_cross_layer_kernel(
                                 rhs=xq[c, hf][:, cols].bitcast(FP8X4), rhs_scale=xs[c, hf][:, cols],
                                 start=(c == 0), stop=(c == PASSES - 1))
 
-        def h_on_vector(hf):
+        def quantise_h(hf, mb, woven):
+            cols = slice(mb * P, (mb + 1) * P)
+            nc.vector.quantize_mx(out=hq[hf][:, cols].bitcast(FP8X4), scales=hs[hf][:, cols],
+                                  in_=woven[:].rearrange("p m t -> p (m t)"))
+
+        def project_on_vector(hf):
             woven = []
             for mb in range(HALF // P):
                 cols = slice(mb * P, (mb + 1) * P)
@@ -155,26 +167,39 @@ def tile_list_lowrank_cross_layer_kernel(
                 for t in range(PACK):
                     for c in range(PASSES):
                         h_pass(bank[:, t, :], t, c, hf, cols)
-                woven.append(ring.tile([P, P, PACK], BF16, name="h_woven", align_bytes=64))
+                woven.append(ring.tile([P, P, PACK], BF16, name="h_woven", align_bytes=64, bufs=4))
                 nc.vector.tensor_tensor(out=woven[mb][:], in0=bank[:].rearrange("p t m -> p m t"),
                                         in1=g_sb[:].unsqueeze(1).to_broadcast([P, P, PACK]), op=MULT)
                 if mb > 0:
                     quantise_h(hf, mb - 1, woven[mb - 1])
             quantise_h(hf, HALF // P - 1, woven[-1])
 
-        def quantise_h(hf, mb, woven):
-            cols = slice(mb * P, (mb + 1) * P)
-            nc.vector.quantize_mx(out=hq[hf][:, cols].bitcast(FP8X4), scales=hs[hf][:, cols],
-                                  in_=woven[:].rearrange("p m t -> p (m t)"))
+        def project_on_scalar(hf):
+            planes = keep.tile([P, PACK, HALF], BF16, name="h_planes")
+            for t in range(PACK):
+                bank = h_banks.tile([P, HALF], F32, name="h_bank")
+                for c in range(PASSES):
+                    h_pass(bank[:], t, c, hf, slice(0, HALF))
+                nc.scalar.activation(out=planes[:, t, :], in_=bank[:], func=COPY, scale=g_sb[:, t:t + 1])
+            for cols in (low, high):
+                woven = ring.tile([P, HALF // 2, PACK], BF16, name="h_woven_half", align_bytes=64)
+                nc.scalar.copy(out=woven[:].rearrange("p (m i) t -> p m t i", i=RUN),
+                               in_=planes[:, :, cols].rearrange("p t (m i) -> p m t i", i=RUN))
+                nc.vector.quantize_mx(out=hq[hf][:, cols].bitcast(FP8X4), scales=hs[hf][:, cols],
+                                      in_=woven[:].rearrange("p m t -> p (m t)"))
 
         wdq = [keep.tile([P, P], U32, name="wdq%d" % i, align_bytes=64) for i in range(N_TILES)]
         wds = [keep.tile([P, P], U8, name="wds%d" % i, align_bytes=64) for i in range(N_TILES)]
         wd_woven = {}
+        wd_listed = {}
 
         def gather_wd(i):
             listed = ring.tile([P, S], BF16, name="wd_listed", align_bytes=64)
             nc.vector.tensor_copy(out=listed[:], in_=wd_raw[i][:].indirect(offsets[:]))
-            pairs = listed[:].bitcast(F32)
+            wd_listed[i] = listed
+
+        def turn_wd(i):
+            pairs = wd_listed[i][:].bitcast(F32)
             bank = t_banks.tile([P, 2, P], F32, name="t_bank")
             for u in range(2):
                 nc.tensor.transpose(bank[:, u, :], pairs[:, u:S // 2:2], ident[:])
@@ -196,34 +221,74 @@ def tile_list_lowrank_cross_layer_kernel(
             nc.tensor.matmul_mx(out=bank[:], lhsT=wdq[i][:].bitcast(FP8X4), lhsT_scale=wds[i][:],
                                 rhs=hq[hf][:].bitcast(FP8X4), rhs_scale=hs[hf][:], start=False, stop=True)
             dst = x0_sb[i][:, hf * HALF:(hf + 1) * HALF]
-            nc.vector.scalar_tensor_tensor(out=dst, in0=bank[:], scalar=b_sb[:, c_out, t:t + 1], in1=dst,
+            nc.vector.scalar_tensor_tensor(out=dst, in0=bank[:], scalar=b_sb[c_out][:, t:t + 1], in1=dst,
                                            op0=ADD, op1=MULT)
 
         def add_skip(i, hf):
             c_out, t = i // PACK, i % PACK
             dst = x0_sb[i][:, hf * HALF:(hf + 1) * HALF]
-            nc.vector.scalar_tensor_tensor(out=dst, in0=x_raw[c_out][:, hf, t, :], scalar=a_sb[:, c_out, t:t + 1],
+            nc.vector.scalar_tensor_tensor(out=dst, in0=x_raw[c_out][:, hf, t, :], scalar=a_sb[c_out][:, t:t + 1],
                                            in1=dst, op0=MULT, op1=ADD)
 
-        def store(i, cols):
-            nc.sync.dma_start(out=out_rows[i // PACK][:, i % PACK, cols], in_=x0_sb[i][:, cols])
+        turned = {}
 
-        prepare_x(0)
-        h_on_vector(0)
-        prepare_x(1)
-        h_on_vector(1)
-        gather_wd(0)
-        quantise_wd(0)
+        def add_skip_turned(i, hf):
+            c_out, t = i // PACK, i % PACK
+            scaled = ring.tile([P, HALF], F32, name="x_scaled")
+            nc.scalar.activation(out=scaled[:], in_=x_raw[c_out][:, hf, t, :], func=COPY, scale=a_sb[c_out][:, t:t + 1])
+            bank = h_banks.tile([P, PACK, P], F32, name="h_bank")
+            for mb in range(HALF // P):
+                crossed = x0_sb[i][:, hf * HALF + mb * P:hf * HALF + (mb + 1) * P]
+                nc.tensor.matmul(bank[:, mb, :], lhsT=crossed, rhs=ident[:], is_transpose=True, start=True, stop=False)
+                nc.tensor.matmul(bank[:, mb, :], lhsT=scaled[:, mb * P:(mb + 1) * P], rhs=ident[:],
+                                 is_transpose=True, start=False, stop=True)
+            turned[i] = ring.tile([P, PACK, P], F32, name="out_turned")
+            nc.scalar.copy(out=turned[i][:], in_=bank[:])
+
+        def turn_back(i, hf):
+            bank = h_banks.tile([P, PACK, P], F32, name="h_bank")
+            for mb in range(HALF // P):
+                nc.tensor.transpose(bank[:, mb, :], turned[i][:, mb, :], ident[:])
+            nc.scalar.copy(out=x0_sb[i][:, hf * HALF:(hf + 1) * HALF], in_=bank[:].rearrange("p b m -> p (b m)"))
+
+        def store(first, count, cols):
+            c_out, rows = first // PACK, slice(first % PACK, first % PACK + count)
+            nc.sync.dma_start(out=out_rows[c_out][:, rows, cols], in_=x0_pass[c_out][:, rows, cols])
+
+        on_vector, on_scalar = nc.vector.tensor_copy, nc.scalar.copy
+        prepare_x(0, 0, on_scalar, on_scalar)
+        prepare_x(1, 0, on_vector, on_scalar)
+        project_on_vector(0)
+        prepare_x(0, 1, on_scalar, on_scalar)
+        prepare_x(1, 1, on_scalar, on_scalar)
+        project_on_scalar(1)
+        for i in range(WD_AHEAD):
+            gather_wd(i)
+            turn_wd(i)
+            quantise_wd(i)
+
+        last = N_TILES - 1
+        by_transposes = range(0, last - 1, 2)
         for i in range(N_TILES):
-            last = i + 1 == N_TILES
-            if not last:
-                gather_wd(i + 1)
-            for hf in range(HALVES):
-                cross(i, hf)
-            for hf in range(HALVES):
-                add_skip(i, hf)
-                if last:
-                    store(i, slice(hf * HALF, (hf + 1) * HALF))
-            if not last:
-                store(i, slice(0, M))
-                quantise_wd(i + 1)
+            ahead = i + WD_AHEAD
+            if ahead < N_TILES:
+                gather_wd(ahead)
+            cross(i, 0)
+            cross(i, 1)
+            if ahead < N_TILES:
+                turn_wd(ahead)
+            if i - 1 in by_transposes:
+                turn_back(i - 1, 1)
+            add_skip(i, 0)
+            if i == last:
+                store(i, 1, slice(0, HALF))
+            if i in by_transposes:
+                add_skip_turned(i, 1)
+            else:
+                add_skip(i, 1)
+            if ahead < N_TILES:
+                quantise_wd(ahead)
+            for first, count in STORES:
+                if i == first + count - 1:
+                    store(first, count, slice(0, M))
+        store(last, 1, slice(HALF, M))

@@ -38,12 +38,15 @@ def tile_list_lowrank_cross_layer_kernel(
     with ExitStack() as ctx:
         keep = ctx.enter_context(tc.tile_pool(name="keep", bufs=1))
         ring = ctx.enter_context(tc.tile_pool(name="ring", bufs=2))
-        h_banks = ctx.enter_context(tc.psum_pool(name="h_banks", bufs=3))
-        t_banks = ctx.enter_context(tc.psum_pool(name="t_banks", bufs=1))
-        y_banks = ctx.enter_context(tc.psum_pool(name="y_banks", bufs=4))
+        psum = ctx.enter_context(tc.psum_pool(name="psum", bufs=1))
+        banks = [psum.tile([P, HALF], F32, name="bank%d" % k) for k in range(8)]
+        h_banks = banks[4:]
+
+        def y_bank(i, hf):
+            return banks[2 * (i % 3) + hf]
 
         offsets = keep.tile([P, S // 16], U16, name="offsets")
-        w4_raw = [keep.tile([P, 2 * N], U8, name="w4_raw%d" % c, align_bytes=64) for c in range(PASSES)]
+        w4_raw = keep.tile([P, PASSES, 2 * N], U8, name="w4_raw", align_bytes=64)
         w4s_raw = keep.tile([P, PASSES, N], U8, name="w4s_raw", align_bytes=64)
         tabs_raw = keep.tile([P, T], U8, name="tabs_raw", align_bytes=64)
         tab_raw = [keep.tile([P, T], I32, name="tab_raw%d" % c, align_bytes=64) for c in range(PASSES)]
@@ -53,7 +56,8 @@ def tile_list_lowrank_cross_layer_kernel(
         x0_sb = [x0_pass[i // PACK][:, i % PACK, :] for i in range(N_TILES)]
         g_sb = keep.tile([P, PACK], F32, name="g_sb")
         a_sb = [keep.tile([P, PACK], F32, name="a_sb%d" % c) for c in range(PASSES)]
-        b_sb = [keep.tile([P, PACK], F32, name="b_sb%d" % c) for c in range(PASSES)]
+        b_all = keep.tile([P, PASSES, PACK], F32, name="b_all")
+        b_sb = [b_all[:, c, :] for c in range(PASSES)]
         ident = keep.tile([P, P], F32, name="ident")
 
         nc.vector.memset(w4s_raw[:].rearrange("p c n -> p (c n)").bitcast(I32), 0)
@@ -74,24 +78,27 @@ def tile_list_lowrank_cross_layer_kernel(
         def load_x0(i):
             nc.sync.dma_start(out=x0_sb[i], in_=x0_rows[i // PACK][:, i % PACK, :])
 
+        def load_tab(c):
+            nc.sync.dma_start(out=tab_raw[c][:], in_=tab_words[c].rearrange("p n t -> p (n t)").bitcast(I32))
+
         nc.sync.dma_start(offsets[:], offs)
         nc.sync.dma_start(out=g_sb[:], in_=g.rearrange("(p t) -> p t", t=PACK))
         for c in range(PASSES):
             nc.sync.dma_start(out=a_sb[c][:], in_=a.rearrange("(c p t) -> c p t", p=P, t=PACK)[c])
-            nc.sync.dma_start(out=b_sb[c][:], in_=b.rearrange("(c p t) -> c p t", p=P, t=PACK)[c])
-        for c in range(PASSES):
-            nc.sync.dma_start(out=w4_raw[c][:].bitcast(I32), in_=w4_words[c].bitcast(I32))
-        for q in QUADRANTS:
-            nc.sync.dma_start(out=w4s_raw[32 * q:32 * q + 4].bitcast(I32),
-                              in_=w4_scales[:, 4 * q:4 * q + 4, :].rearrange("c r n -> r c n").bitcast(I32))
-        nc.sync.dma_start(out=tab_raw[0][:], in_=tab_words[0].rearrange("p n t -> p (n t)").bitcast(I32))
+        nc.sync.dma_start(out=b_all[:], in_=b.rearrange("(c p t) -> p c t", p=P, t=PACK))
+        nc.sync.dma_start(out=w4_raw[:].bitcast(I32), in_=w4_words.rearrange("c p n -> p c n").bitcast(I32))
+        load_x(0, 0)
+        load_tab(0)
         for q in QUADRANTS:
             nc.sync.dma_start(out=tabs_raw[32 * q:32 * q + 8, :].bitcast(I32),
                               in_=tab_scales[:, 4 * q:4 * q + 4, :].bitcast(I32))
-        nc.sync.dma_start(out=tab_raw[1][:], in_=tab_words[1].rearrange("p n t -> p (n t)").bitcast(I32))
-        for hf in range(HALVES):
-            for c in range(PASSES):
-                load_x(c, hf)
+        load_tab(1)
+        for q in QUADRANTS:
+            nc.sync.dma_start(out=w4s_raw[32 * q:32 * q + 4].bitcast(I32),
+                              in_=w4_scales[:, 4 * q:4 * q + 4, :].rearrange("c r n -> r c n").bitcast(I32))
+        load_x(1, 0)
+        load_x(0, 1)
+        load_x(1, 1)
         for i in range(WD_AHEAD):
             load_wd(i)
         for i in range(N_TILES):
@@ -104,10 +111,7 @@ def tile_list_lowrank_cross_layer_kernel(
         for c in range(PASSES):
             nc.vector.tensor_copy(
                 out=w4q[:, c, :].bitcast(U16).rearrange("p (d t q) -> p d t q", t=PACK, q=P),
-                in_=w4_raw[c][:].bitcast(U16).rearrange("p (d q t) -> p d t q", t=PACK, q=P))
-        nc.vector.tensor_copy(
-            out=w4s[:].rearrange("p c (d t q) -> p (c d) t q", t=PACK, q=P),
-            in_=w4s_raw[:].rearrange("p c (d q t) -> p (c d) t q", t=PACK, q=P))
+                in_=w4_raw[:, c, :].bitcast(U16).rearrange("p (d q t) -> p d t q", t=PACK, q=P))
 
         vq = [keep.tile([P, S], U32, name="vq%d" % c, align_bytes=64) for c in range(PASSES)]
         vs_listed = keep.tile([P, S], U8, name="vs_listed", align_bytes=64)
@@ -115,10 +119,13 @@ def tile_list_lowrank_cross_layer_kernel(
         nc.vector.tensor_copy(out=vq[0][:].rearrange("p (t q) -> p q t", t=PACK),
                               in_=tab_raw[0][:].bitcast(U32).indirect(offsets[:]))
         nc.vector.tensor_copy(out=vs_listed[:], in_=tabs_raw[:].indirect(offsets[:]))
-        nc.vector.tensor_copy(out=vq[1][:].rearrange("p (t q) -> p q t", t=PACK),
-                              in_=tab_raw[1][:].bitcast(U32).indirect(offsets[:]))
         nc.vector.tensor_copy(out=vs[:].rearrange("p (t q) -> p t q", t=PACK),
                               in_=vs_listed[:].rearrange("p (q t) -> p t q", t=PACK))
+        nc.vector.tensor_copy(out=vq[1][:].rearrange("p (t q) -> p q t", t=PACK),
+                              in_=tab_raw[1][:].bitcast(U32).indirect(offsets[:]))
+        nc.vector.tensor_copy(
+            out=w4s[:].rearrange("p c (d t q) -> p (c d) t q", t=PACK, q=P),
+            in_=w4s_raw[:].rearrange("p c (d q t) -> p (c d) t q", t=PACK, q=P))
 
         xq = {}
         xs = {}
@@ -127,23 +134,17 @@ def tile_list_lowrank_cross_layer_kernel(
                 xq[c, hf] = keep.tile([P, HALF], U32, name="xq%d%d" % (c, hf), align_bytes=64)
                 xs[c, hf] = keep.tile([P, HALF], U8, name="xs%d%d" % (c, hf), align_bytes=64)
 
-        def weave_x(copy, c, hf, cols):
-            woven = ring.tile([P, cols.stop - cols.start, PACK], BF16, name="x_woven", align_bytes=64, bufs=6)
-            copy(out=woven[:].rearrange("p (m i) t -> p m t i", i=RUN),
-                 in_=x_raw[c][:, hf, :, cols].rearrange("p t (m i) -> p m t i", i=RUN))
-            return woven
+        low, high, whole = slice(0, HALF // 2), slice(HALF // 2, HALF), slice(0, HALF)
 
-        def quantise_x(woven, c, hf, cols):
-            nc.vector.quantize_mx(out=xq[c, hf][:, cols].bitcast(FP8X4), scales=xs[c, hf][:, cols],
-                                  in_=woven[:].rearrange("p m t -> p (m t)"))
+        def weave(copy, woven, rows, cols):
+            copy(out=woven[:, cols.start * PACK:cols.stop * PACK].rearrange("p (m i t) -> p m t i", i=RUN, t=PACK),
+                 in_=rows[:, :, cols].rearrange("p t (m i) -> p m t i", i=RUN))
 
-        low, high = slice(0, HALF // 2), slice(HALF // 2, HALF)
-
-        def prepare_x(c, hf, copy_low, copy_high):
-            first = weave_x(copy_low, c, hf, low)
-            second = weave_x(copy_high, c, hf, high)
-            quantise_x(first, c, hf, low)
-            quantise_x(second, c, hf, high)
+        def prepare_x(c, hf, shares):
+            woven = ring.tile([P, HALF * PACK], BF16, name="woven", align_bytes=64, bufs=3)
+            for copy, cols in shares:
+                weave(copy, woven, x_raw[c][:, hf], cols)
+            nc.vector.quantize_mx(out=xq[c, hf][:].bitcast(FP8X4), scales=xs[c, hf][:], in_=woven[:])
 
         hq = [keep.tile([P, HALF], U32, name="hq%d" % hf, align_bytes=64) for hf in range(HALVES)]
         hs = [keep.tile([P, HALF], U8, name="hs%d" % hf, align_bytes=64) for hf in range(HALVES)]
@@ -154,65 +155,49 @@ def tile_list_lowrank_cross_layer_kernel(
                                 rhs=xq[c, hf][:, cols].bitcast(FP8X4), rhs_scale=xs[c, hf][:, cols],
                                 start=(c == 0), stop=(c == PASSES - 1))
 
-        def quantise_h(hf, mb, woven):
-            cols = slice(mb * P, (mb + 1) * P)
-            nc.vector.quantize_mx(out=hq[hf][:, cols].bitcast(FP8X4), scales=hs[hf][:, cols],
-                                  in_=woven[:].rearrange("p m t -> p (m t)"))
-
-        def project_on_vector(hf):
-            woven = []
-            for mb in range(HALF // P):
-                cols = slice(mb * P, (mb + 1) * P)
-                bank = h_banks.tile([P, PACK, P], F32, name="h_bank")
-                for t in range(PACK):
-                    for c in range(PASSES):
-                        h_pass(bank[:, t, :], t, c, hf, cols)
-                woven.append(ring.tile([P, P, PACK], BF16, name="h_woven", align_bytes=64, bufs=4))
-                nc.vector.tensor_tensor(out=woven[mb][:], in0=bank[:].rearrange("p t m -> p m t"),
-                                        in1=g_sb[:].unsqueeze(1).to_broadcast([P, P, PACK]), op=MULT)
-                if mb > 0:
-                    quantise_h(hf, mb - 1, woven[mb - 1])
-            quantise_h(hf, HALF // P - 1, woven[-1])
-
-        def project_on_scalar(hf):
-            planes = keep.tile([P, PACK, HALF], BF16, name="h_planes")
+        def project(hf, copy, parts):
+            planes = ring.tile([P, PACK, HALF], BF16, name="h_planes")
+            woven = ring.tile([P, HALF * PACK], BF16, name="woven", align_bytes=64, bufs=3)
             for t in range(PACK):
-                bank = h_banks.tile([P, HALF], F32, name="h_bank")
+                bank = h_banks[t]
                 for c in range(PASSES):
-                    h_pass(bank[:], t, c, hf, slice(0, HALF))
+                    h_pass(bank[:], t, c, hf, whole)
                 nc.scalar.activation(out=planes[:, t, :], in_=bank[:], func=COPY, scale=g_sb[:, t:t + 1])
-            for cols in (low, high):
-                woven = ring.tile([P, HALF // 2, PACK], BF16, name="h_woven_half", align_bytes=64)
-                nc.scalar.copy(out=woven[:].rearrange("p (m i) t -> p m t i", i=RUN),
-                               in_=planes[:, :, cols].rearrange("p t (m i) -> p m t i", i=RUN))
+            for cols in parts:
+                weave(copy, woven, planes, cols)
+            for cols in parts:
                 nc.vector.quantize_mx(out=hq[hf][:, cols].bitcast(FP8X4), scales=hs[hf][:, cols],
-                                      in_=woven[:].rearrange("p m t -> p (m t)"))
+                                      in_=woven[:, cols.start * PACK:cols.stop * PACK])
 
         wdq = [keep.tile([P, P], U32, name="wdq%d" % i, align_bytes=64) for i in range(N_TILES)]
         wds = [keep.tile([P, P], U8, name="wds%d" % i, align_bytes=64) for i in range(N_TILES)]
         wd_woven = {}
         wd_listed = {}
 
+        listed_tiles = [keep.tile([P, S], BF16, name="wd_listed%d" % r, align_bytes=64) for r in range(2)]
+        last = N_TILES - 1
+
         def gather_wd(i):
-            listed = ring.tile([P, S], BF16, name="wd_listed", align_bytes=64)
-            nc.vector.tensor_copy(out=listed[:], in_=wd_raw[i][:].indirect(offsets[:]))
+            listed = listed_tiles[i % 2][:]
+            nc.vector.tensor_copy(out=listed, in_=wd_raw[i][:].indirect(offsets[:]))
             wd_listed[i] = listed
 
         def turn_wd(i):
-            pairs = wd_listed[i][:].bitcast(F32)
-            bank = t_banks.tile([P, 2, P], F32, name="t_bank")
+            pairs = wd_listed[i].bitcast(F32)
+            whole_bank = banks[6 + i % 2]
+            bank = whole_bank[:, :2 * P].rearrange("p (u n) -> p u n", u=2)
             for u in range(2):
                 nc.tensor.transpose(bank[:, u, :], pairs[:, u:S // 2:2], ident[:])
             wd_woven[i] = ring.tile([P, P * PACK], BF16, name="wd_woven", align_bytes=64)
             nc.scalar.copy(out=wd_woven[i][:].bitcast(F32).rearrange("p (n u) -> p n u", u=2),
-                           in_=bank[:].rearrange("p u n -> p n u"))
+                           in_=bank.rearrange("p u n -> p n u"))
 
         def quantise_wd(i):
             nc.vector.quantize_mx(out=wdq[i][:].bitcast(FP8X4), scales=wds[i][:], in_=wd_woven[i][:])
 
         def cross(i, hf):
             c_out, t = i // PACK, i % PACK
-            bank = y_banks.tile([P, HALF], F32, name="y_bank")
+            bank = y_bank(i, hf)
             for c in range(PASSES):
                 nc.tensor.matmul_mx(out=bank[:], lhsT=w4q[:, c, 2 * i * P:2 * (i + 1) * P].bitcast(FP4X4),
                                     lhsT_scale=w4s[:, c, i * P:(i + 1) * P],
@@ -220,9 +205,9 @@ def tile_list_lowrank_cross_layer_kernel(
                                     start=(c == 0), stop=False)
             nc.tensor.matmul_mx(out=bank[:], lhsT=wdq[i][:].bitcast(FP8X4), lhsT_scale=wds[i][:],
                                 rhs=hq[hf][:].bitcast(FP8X4), rhs_scale=hs[hf][:], start=False, stop=True)
-            dst = x0_sb[i][:, hf * HALF:(hf + 1) * HALF]
-            nc.vector.scalar_tensor_tensor(out=dst, in0=bank[:], scalar=b_sb[c_out][:, t:t + 1], in1=dst,
-                                           op0=ADD, op1=MULT)
+            cols = slice(hf * HALF, (hf + 1) * HALF)
+            nc.vector.scalar_tensor_tensor(out=x0_sb[i][:, cols], in0=bank[:], scalar=b_sb[c_out][:, t:t + 1],
+                                           in1=x0_sb[i][:, cols], op0=ADD, op1=MULT)
 
         def add_skip(i, hf):
             c_out, t = i // PACK, i % PACK
@@ -230,45 +215,29 @@ def tile_list_lowrank_cross_layer_kernel(
             nc.vector.scalar_tensor_tensor(out=dst, in0=x_raw[c_out][:, hf, t, :], scalar=a_sb[c_out][:, t:t + 1],
                                            in1=dst, op0=MULT, op1=ADD)
 
-        turned = {}
-
-        def add_skip_turned(i, hf):
+        def add_skip_aside(i, hf):
             c_out, t = i // PACK, i % PACK
-            scaled = ring.tile([P, HALF], F32, name="x_scaled")
-            nc.scalar.activation(out=scaled[:], in_=x_raw[c_out][:, hf, t, :], func=COPY, scale=a_sb[c_out][:, t:t + 1])
-            bank = h_banks.tile([P, PACK, P], F32, name="h_bank")
-            for mb in range(HALF // P):
-                crossed = x0_sb[i][:, hf * HALF + mb * P:hf * HALF + (mb + 1) * P]
-                nc.tensor.matmul(bank[:, mb, :], lhsT=crossed, rhs=ident[:], is_transpose=True, start=True, stop=False)
-                nc.tensor.matmul(bank[:, mb, :], lhsT=scaled[:, mb * P:(mb + 1) * P], rhs=ident[:],
-                                 is_transpose=True, start=False, stop=True)
-            turned[i] = ring.tile([P, PACK, P], F32, name="out_turned")
-            nc.scalar.copy(out=turned[i][:], in_=bank[:])
-
-        def turn_back(i, hf):
-            bank = h_banks.tile([P, PACK, P], F32, name="h_bank")
-            for mb in range(HALF // P):
-                nc.tensor.transpose(bank[:, mb, :], turned[i][:, mb, :], ident[:])
-            nc.scalar.copy(out=x0_sb[i][:, hf * HALF:(hf + 1) * HALF], in_=bank[:].rearrange("p b m -> p (b m)"))
+            rows = x_raw[c_out][:, hf, t, :]
+            nc.scalar.activation(out=rows, in_=rows, func=COPY, scale=a_sb[c_out][:, t:t + 1])
+            cols = slice(hf * HALF, (hf + 1) * HALF)
+            nc.gpsimd.tensor_tensor(out=x0_sb[i][:, cols], in0=x0_sb[i][:, cols], in1=rows, op=ADD)
 
         def store(first, count, cols):
             c_out, rows = first // PACK, slice(first % PACK, first % PACK + count)
             nc.sync.dma_start(out=out_rows[c_out][:, rows, cols], in_=x0_pass[c_out][:, rows, cols])
 
         on_vector, on_scalar = nc.vector.tensor_copy, nc.scalar.copy
-        prepare_x(0, 0, on_scalar, on_scalar)
-        prepare_x(1, 0, on_vector, on_scalar)
-        project_on_vector(0)
-        prepare_x(0, 1, on_scalar, on_scalar)
-        prepare_x(1, 1, on_scalar, on_scalar)
-        project_on_scalar(1)
+        prepare_x(0, 0, ((on_scalar, whole),))
+        prepare_x(1, 0, ((on_vector, low), (on_scalar, high)))
+        prepare_x(0, 1, ((on_vector, whole),))
+        prepare_x(1, 1, ((on_vector, whole),))
+        project(0, on_scalar, (whole,))
+        project(1, on_vector, (low, high))
         for i in range(WD_AHEAD):
             gather_wd(i)
             turn_wd(i)
             quantise_wd(i)
 
-        last = N_TILES - 1
-        by_transposes = range(0, last - 1, 2)
         for i in range(N_TILES):
             ahead = i + WD_AHEAD
             if ahead < N_TILES:
@@ -277,18 +246,19 @@ def tile_list_lowrank_cross_layer_kernel(
             cross(i, 1)
             if ahead < N_TILES:
                 turn_wd(ahead)
-            if i - 1 in by_transposes:
-                turn_back(i - 1, 1)
-            add_skip(i, 0)
-            if i == last:
-                store(i, 1, slice(0, HALF))
-            if i in by_transposes:
-                add_skip_turned(i, 1)
-            else:
-                add_skip(i, 1)
-            if ahead < N_TILES:
                 quantise_wd(ahead)
-            for first, count in STORES:
-                if i == first + count - 1:
-                    store(first, count, slice(0, M))
-        store(last, 1, slice(HALF, M))
+            if i < last - 1:
+                add_skip_aside(i, 0)
+                add_skip_aside(i, 1)
+            elif i < last:
+                add_skip(i, 0)
+                add_skip(i, 1)
+            else:
+                add_skip(i, 0)
+                store(i, 1, slice(0, HALF))
+                add_skip(i, 1)
+                store(i, 1, slice(HALF, M))
+            if i in (1, 3, 5):
+                store(i - 1, 2, slice(0, M))
+            if i == last - 1:
+                store(i, 1, slice(0, M))

@@ -43,7 +43,7 @@ def tile_list_lowrank_cross_layer_kernel(
         h_banks = banks[4:]
 
         def y_bank(i, hf):
-            return banks[2 * (i % 3) + hf]
+            return banks[2 * (i % 2) + hf]
 
         offsets = keep.tile([P, S // 16], U16, name="offsets")
         w4_raw = keep.tile([P, PASSES, 2 * N], U8, name="w4_raw", align_bytes=64)
@@ -215,12 +215,25 @@ def tile_list_lowrank_cross_layer_kernel(
             nc.vector.scalar_tensor_tensor(out=dst, in0=x_raw[c_out][:, hf, t, :], scalar=a_sb[c_out][:, t:t + 1],
                                            in1=dst, op0=MULT, op1=ADD)
 
-        def add_skip_aside(i, hf):
+        turned = keep.tile([P, HALF], F32, name="turned")
+
+        def add_skip_turned(i, hf):
             c_out, t = i // PACK, i % PACK
             rows = x_raw[c_out][:, hf, t, :]
             nc.scalar.activation(out=rows, in_=rows, func=COPY, scale=a_sb[c_out][:, t:t + 1])
-            cols = slice(hf * HALF, (hf + 1) * HALF)
-            nc.gpsimd.tensor_tensor(out=x0_sb[i][:, cols], in0=x0_sb[i][:, cols], in1=rows, op=ADD)
+            for mb in range(HALF // P):
+                block = slice(mb * P, (mb + 1) * P)
+                nc.tensor.matmul(banks[4][:, block], lhsT=x0_sb[i][:, hf * HALF + mb * P:hf * HALF + (mb + 1) * P],
+                                 rhs=ident[:], is_transpose=True, start=True, stop=False)
+                nc.tensor.matmul(banks[4][:, block], lhsT=rows[:, block], rhs=ident[:],
+                                 is_transpose=True, start=False, stop=True)
+            nc.scalar.copy(out=turned[:], in_=banks[4][:])
+
+        def turn_back(i, hf):
+            for mb in range(HALF // P):
+                block = slice(mb * P, (mb + 1) * P)
+                nc.tensor.transpose(banks[5][:, block], turned[:, block], ident[:])
+            nc.scalar.copy(out=x0_sb[i][:, hf * HALF:(hf + 1) * HALF], in_=banks[5][:])
 
         def store(first, count, cols):
             c_out, rows = first // PACK, slice(first % PACK, first % PACK + count)
@@ -238,6 +251,7 @@ def tile_list_lowrank_cross_layer_kernel(
             turn_wd(i)
             quantise_wd(i)
 
+        by_transposes = range(0, last - 1, 2)
         for i in range(N_TILES):
             ahead = i + WD_AHEAD
             if ahead < N_TILES:
@@ -246,19 +260,19 @@ def tile_list_lowrank_cross_layer_kernel(
             cross(i, 1)
             if ahead < N_TILES:
                 turn_wd(ahead)
-                quantise_wd(ahead)
-            if i < last - 1:
-                add_skip_aside(i, 0)
-                add_skip_aside(i, 1)
-            elif i < last:
-                add_skip(i, 0)
-                add_skip(i, 1)
-            else:
-                add_skip(i, 0)
+            if i - 1 in by_transposes:
+                turn_back(i - 1, 1)
+            add_skip(i, 0)
+            if i == last:
                 store(i, 1, slice(0, HALF))
+            if i in by_transposes:
+                add_skip_turned(i, 1)
+            else:
                 add_skip(i, 1)
-                store(i, 1, slice(HALF, M))
+            if ahead < N_TILES:
+                quantise_wd(ahead)
             if i in (1, 3, 5):
                 store(i - 1, 2, slice(0, M))
             if i == last - 1:
                 store(i, 1, slice(0, M))
+        store(last, 1, slice(HALF, M))

@@ -81,12 +81,12 @@ def tile_list_lowrank_cross_layer_kernel(
         def load_tab(c):
             nc.sync.dma_start(out=tab_raw[c][:], in_=tab_words[c].rearrange("p n t -> p (n t)").bitcast(I32))
 
+        nc.sync.dma_start(out=w4_raw[:].bitcast(I32), in_=w4_words.rearrange("c p n -> p c n").bitcast(I32))
         nc.sync.dma_start(offsets[:], offs)
         nc.sync.dma_start(out=g_sb[:], in_=g.rearrange("(p t) -> p t", t=PACK))
         for c in range(PASSES):
             nc.sync.dma_start(out=a_sb[c][:], in_=a.rearrange("(c p t) -> c p t", p=P, t=PACK)[c])
         nc.sync.dma_start(out=b_all[:], in_=b.rearrange("(c p t) -> p c t", p=P, t=PACK))
-        nc.sync.dma_start(out=w4_raw[:].bitcast(I32), in_=w4_words.rearrange("c p n -> p c n").bitcast(I32))
         load_x(0, 0)
         load_tab(0)
         for q in QUADRANTS:
@@ -251,7 +251,7 @@ def tile_list_lowrank_cross_layer_kernel(
             turn_wd(i)
             quantise_wd(i)
 
-        by_transposes = range(0, last - 1, 2)
+        by_transposes = range(2, last - 1, 2)
         for i in range(N_TILES):
             ahead = i + WD_AHEAD
             if ahead < N_TILES:

@@ -28,7 +28,7 @@ N_TILES = N // P
 WD_AHEAD = 2
 RUN = 4
 QUADRANTS = (0, 2, 1, 3)
-STORES = ((0, 4), (4, 2), (6, 1))
+WOVEN_BUFS = 3
 
 
 def tile_list_lowrank_cross_layer_kernel(
@@ -41,6 +41,8 @@ def tile_list_lowrank_cross_layer_kernel(
         psum = ctx.enter_context(tc.psum_pool(name="psum", bufs=1))
         banks = [psum.tile([P, HALF], F32, name="bank%d" % k) for k in range(8)]
         h_banks = banks[4:]
+        sum_bank, back_bank = banks[4:6]
+        wd_banks = banks[6:]
 
         def y_bank(i, hf):
             return banks[2 * (i % 2) + hf]
@@ -55,7 +57,8 @@ def tile_list_lowrank_cross_layer_kernel(
         x0_pass = [keep.tile([P, PACK, M], F32, name="x0_pass%d" % c) for c in range(PASSES)]
         x0_sb = [x0_pass[i // PACK][:, i % PACK, :] for i in range(N_TILES)]
         g_sb = keep.tile([P, PACK], F32, name="g_sb")
-        a_sb = [keep.tile([P, PACK], F32, name="a_sb%d" % c) for c in range(PASSES)]
+        a_all = keep.tile([P, PASSES, PACK], F32, name="a_all")
+        a_sb = [a_all[:, c, :] for c in range(PASSES)]
         b_all = keep.tile([P, PASSES, PACK], F32, name="b_all")
         b_sb = [b_all[:, c, :] for c in range(PASSES)]
         ident = keep.tile([P, P], F32, name="ident")
@@ -75,8 +78,9 @@ def tile_list_lowrank_cross_layer_kernel(
         def load_wd(i):
             nc.sync.dma_start(out=wd_raw[i][:], in_=wd_rows[i // PACK][i % PACK])
 
-        def load_x0(i):
-            nc.sync.dma_start(out=x0_sb[i], in_=x0_rows[i // PACK][:, i % PACK, :])
+        def load_x0(first, count):
+            rows = slice(first % PACK, first % PACK + count)
+            nc.sync.dma_start(out=x0_pass[first // PACK][:, rows, :], in_=x0_rows[first // PACK][:, rows, :])
 
         def load_tab(c):
             nc.sync.dma_start(out=tab_raw[c][:], in_=tab_words[c].rearrange("p n t -> p (n t)").bitcast(I32))
@@ -84,27 +88,26 @@ def tile_list_lowrank_cross_layer_kernel(
         nc.sync.dma_start(out=w4_raw[:].bitcast(I32), in_=w4_words.rearrange("c p n -> p c n").bitcast(I32))
         nc.sync.dma_start(offsets[:], offs)
         nc.sync.dma_start(out=g_sb[:], in_=g.rearrange("(p t) -> p t", t=PACK))
-        for c in range(PASSES):
-            nc.sync.dma_start(out=a_sb[c][:], in_=a.rearrange("(c p t) -> c p t", p=P, t=PACK)[c])
+        nc.sync.dma_start(out=a_all[:], in_=a.rearrange("(c p t) -> p c t", p=P, t=PACK))
         nc.sync.dma_start(out=b_all[:], in_=b.rearrange("(c p t) -> p c t", p=P, t=PACK))
         load_x(0, 0)
         load_tab(0)
+        load_tab(1)
         for q in QUADRANTS:
             nc.sync.dma_start(out=tabs_raw[32 * q:32 * q + 8, :].bitcast(I32),
                               in_=tab_scales[:, 4 * q:4 * q + 4, :].bitcast(I32))
-        load_tab(1)
+        load_x(1, 0)
         for q in QUADRANTS:
             nc.sync.dma_start(out=w4s_raw[32 * q:32 * q + 4].bitcast(I32),
                               in_=w4_scales[:, 4 * q:4 * q + 4, :].rearrange("c r n -> r c n").bitcast(I32))
-        load_x(1, 0)
         load_x(0, 1)
         load_x(1, 1)
         for i in range(WD_AHEAD):
             load_wd(i)
-        for i in range(N_TILES):
-            if i + WD_AHEAD < N_TILES:
-                load_wd(i + WD_AHEAD)
-            load_x0(i)
+        for i in range(N_TILES - WD_AHEAD):
+            load_wd(i + WD_AHEAD)
+            load_x0(i, 1)
+        load_x0(N_TILES - WD_AHEAD, WD_AHEAD)
 
         w4q = keep.tile([P, PASSES, 2 * N], U8, name="w4q", align_bytes=64)
         w4s = keep.tile([P, PASSES, N], U8, name="w4s", align_bytes=64)
@@ -116,16 +119,12 @@ def tile_list_lowrank_cross_layer_kernel(
         vq = [keep.tile([P, S], U32, name="vq%d" % c, align_bytes=64) for c in range(PASSES)]
         vs_listed = keep.tile([P, S], U8, name="vs_listed", align_bytes=64)
         vs = keep.tile([P, S], U8, name="vs", align_bytes=64)
-        nc.vector.tensor_copy(out=vq[0][:].rearrange("p (t q) -> p q t", t=PACK),
-                              in_=tab_raw[0][:].bitcast(U32).indirect(offsets[:]))
+        for c in range(PASSES):
+            nc.vector.tensor_copy(out=vq[c][:].rearrange("p (t q) -> p q t", t=PACK),
+                                  in_=tab_raw[c][:].bitcast(U32).indirect(offsets[:]))
         nc.vector.tensor_copy(out=vs_listed[:], in_=tabs_raw[:].indirect(offsets[:]))
         nc.vector.tensor_copy(out=vs[:].rearrange("p (t q) -> p t q", t=PACK),
                               in_=vs_listed[:].rearrange("p (q t) -> p t q", t=PACK))
-        nc.vector.tensor_copy(out=vq[1][:].rearrange("p (t q) -> p q t", t=PACK),
-                              in_=tab_raw[1][:].bitcast(U32).indirect(offsets[:]))
-        nc.vector.tensor_copy(
-            out=w4s[:].rearrange("p c (d t q) -> p (c d) t q", t=PACK, q=P),
-            in_=w4s_raw[:].rearrange("p c (d q t) -> p (c d) t q", t=PACK, q=P))
 
         xq = {}
         xs = {}
@@ -141,7 +140,7 @@ def tile_list_lowrank_cross_layer_kernel(
                  in_=rows[:, :, cols].rearrange("p t (m i) -> p m t i", i=RUN))
 
         def prepare_x(c, hf, shares):
-            woven = ring.tile([P, HALF * PACK], BF16, name="woven", align_bytes=64, bufs=3)
+            woven = ring.tile([P, HALF * PACK], BF16, name="woven", align_bytes=64, bufs=WOVEN_BUFS)
             for copy, cols in shares:
                 weave(copy, woven, x_raw[c][:, hf], cols)
             nc.vector.quantize_mx(out=xq[c, hf][:].bitcast(FP8X4), scales=xs[c, hf][:], in_=woven[:])
@@ -149,19 +148,16 @@ def tile_list_lowrank_cross_layer_kernel(
         hq = [keep.tile([P, HALF], U32, name="hq%d" % hf, align_bytes=64) for hf in range(HALVES)]
         hs = [keep.tile([P, HALF], U8, name="hs%d" % hf, align_bytes=64) for hf in range(HALVES)]
 
-        def h_pass(dst, t, c, hf, cols):
-            nc.tensor.matmul_mx(out=dst, lhsT=vq[c][:, t * P:(t + 1) * P].bitcast(FP8X4),
-                                lhsT_scale=vs[4 * c:, t * P:(t + 1) * P],
-                                rhs=xq[c, hf][:, cols].bitcast(FP8X4), rhs_scale=xs[c, hf][:, cols],
-                                start=(c == 0), stop=(c == PASSES - 1))
-
         def project(hf, copy, parts):
             planes = ring.tile([P, PACK, HALF], BF16, name="h_planes")
-            woven = ring.tile([P, HALF * PACK], BF16, name="woven", align_bytes=64, bufs=3)
+            woven = ring.tile([P, HALF * PACK], BF16, name="woven", align_bytes=64, bufs=WOVEN_BUFS)
             for t in range(PACK):
                 bank = h_banks[t]
                 for c in range(PASSES):
-                    h_pass(bank[:], t, c, hf, whole)
+                    nc.tensor.matmul_mx(out=bank[:], lhsT=vq[c][:, t * P:(t + 1) * P].bitcast(FP8X4),
+                                        lhsT_scale=vs[4 * c:, t * P:(t + 1) * P],
+                                        rhs=xq[c, hf][:].bitcast(FP8X4), rhs_scale=xs[c, hf][:],
+                                        start=(c == 0), stop=(c == PASSES - 1))
                 nc.scalar.activation(out=planes[:, t, :], in_=bank[:], func=COPY, scale=g_sb[:, t:t + 1])
             for cols in parts:
                 weave(copy, woven, planes, cols)
@@ -172,20 +168,14 @@ def tile_list_lowrank_cross_layer_kernel(
         wdq = [keep.tile([P, P], U32, name="wdq%d" % i, align_bytes=64) for i in range(N_TILES)]
         wds = [keep.tile([P, P], U8, name="wds%d" % i, align_bytes=64) for i in range(N_TILES)]
         wd_woven = {}
-        wd_listed = {}
-
-        listed_tiles = [keep.tile([P, S], BF16, name="wd_listed%d" % r, align_bytes=64) for r in range(2)]
-        last = N_TILES - 1
+        wd_listed = [keep.tile([P, S], BF16, name="wd_listed%d" % r, align_bytes=64) for r in range(2)]
 
         def gather_wd(i):
-            listed = listed_tiles[i % 2][:]
-            nc.vector.tensor_copy(out=listed, in_=wd_raw[i][:].indirect(offsets[:]))
-            wd_listed[i] = listed
+            nc.vector.tensor_copy(out=wd_listed[i % 2][:], in_=wd_raw[i][:].indirect(offsets[:]))
 
         def turn_wd(i):
-            pairs = wd_listed[i].bitcast(F32)
-            whole_bank = banks[6 + i % 2]
-            bank = whole_bank[:, :2 * P].rearrange("p (u n) -> p u n", u=2)
+            pairs = wd_listed[i % 2][:].bitcast(F32)
+            bank = wd_banks[i % 2][:, :2 * P].rearrange("p (u n) -> p u n", u=2)
             for u in range(2):
                 nc.tensor.transpose(bank[:, u, :], pairs[:, u:S // 2:2], ident[:])
             wd_woven[i] = ring.tile([P, P * PACK], BF16, name="wd_woven", align_bytes=64)
@@ -219,21 +209,21 @@ def tile_list_lowrank_cross_layer_kernel(
 
         def add_skip_turned(i, hf):
             c_out, t = i // PACK, i % PACK
-            rows = x_raw[c_out][:, hf, t, :]
-            nc.scalar.activation(out=rows, in_=rows, func=COPY, scale=a_sb[c_out][:, t:t + 1])
+            scaled = x_raw[c_out][:, hf, t, :]
+            nc.scalar.activation(out=scaled, in_=scaled, func=COPY, scale=a_sb[c_out][:, t:t + 1])
             for mb in range(HALF // P):
                 block = slice(mb * P, (mb + 1) * P)
-                nc.tensor.matmul(banks[4][:, block], lhsT=x0_sb[i][:, hf * HALF + mb * P:hf * HALF + (mb + 1) * P],
+                nc.tensor.matmul(sum_bank[:, block], lhsT=x0_sb[i][:, hf * HALF + mb * P:hf * HALF + (mb + 1) * P],
                                  rhs=ident[:], is_transpose=True, start=True, stop=False)
-                nc.tensor.matmul(banks[4][:, block], lhsT=rows[:, block], rhs=ident[:],
+                nc.tensor.matmul(sum_bank[:, block], lhsT=scaled[:, block], rhs=ident[:],
                                  is_transpose=True, start=False, stop=True)
-            nc.scalar.copy(out=turned[:], in_=banks[4][:])
+            nc.scalar.copy(out=turned[:], in_=sum_bank[:])
 
         def turn_back(i, hf):
             for mb in range(HALF // P):
                 block = slice(mb * P, (mb + 1) * P)
-                nc.tensor.transpose(banks[5][:, block], turned[:, block], ident[:])
-            nc.scalar.copy(out=x0_sb[i][:, hf * HALF:(hf + 1) * HALF], in_=banks[5][:])
+                nc.tensor.transpose(back_bank[:, block], turned[:, block], ident[:])
+            nc.scalar.copy(out=x0_sb[i][:, hf * HALF:(hf + 1) * HALF], in_=back_bank[:])
 
         def store(first, count, cols):
             c_out, rows = first // PACK, slice(first % PACK, first % PACK + count)
@@ -242,6 +232,9 @@ def tile_list_lowrank_cross_layer_kernel(
         on_vector, on_scalar = nc.vector.tensor_copy, nc.scalar.copy
         prepare_x(0, 0, ((on_scalar, whole),))
         prepare_x(1, 0, ((on_vector, low), (on_scalar, high)))
+        nc.vector.tensor_copy(
+            out=w4s[:].rearrange("p c (d t q) -> p (c d) t q", t=PACK, q=P),
+            in_=w4s_raw[:].rearrange("p c (d q t) -> p (c d) t q", t=PACK, q=P))
         prepare_x(0, 1, ((on_vector, whole),))
         prepare_x(1, 1, ((on_vector, whole),))
         project(0, on_scalar, (whole,))
@@ -251,6 +244,8 @@ def tile_list_lowrank_cross_layer_kernel(
             turn_wd(i)
             quantise_wd(i)
 
+        last = N_TILES - 1
+        stores = {3: (0, 4), 5: (4, 2), 6: (6, 1)}
         by_transposes = range(2, last - 1, 2)
         for i in range(N_TILES):
             ahead = i + WD_AHEAD
@@ -271,8 +266,6 @@ def tile_list_lowrank_cross_layer_kernel(
                 add_skip(i, 1)
             if ahead < N_TILES:
                 quantise_wd(ahead)
-            if i in (1, 3, 5):
-                store(i - 1, 2, slice(0, M))
-            if i == last - 1:
-                store(i, 1, slice(0, M))
+            if i in stores:
+                store(*stores[i], slice(0, M))
         store(last, 1, slice(HALF, M))

@@ -25,7 +25,7 @@ PASSES = K // K_PASS
 HALF = 512
 HALVES = M // HALF
 N_TILES = N // P
-WD_AHEAD = 2
+WD_AHEAD = 1
 RUN = 4
 QUADRANTS = (0, 2, 1, 3)
 WOVEN_BUFS = 3
@@ -40,8 +40,7 @@ def tile_list_lowrank_cross_layer_kernel(
         ring = ctx.enter_context(tc.tile_pool(name="ring", bufs=2))
         psum = ctx.enter_context(tc.psum_pool(name="psum", bufs=1))
         banks = [psum.tile([P, HALF], F32, name="bank%d" % k) for k in range(8)]
-        h_banks = banks[4:]
-        sum_bank, back_bank = banks[4:6]
+        h_banks = (banks[4:], banks[:4])
         wd_banks = banks[6:]
 
         def y_bank(i, hf):
@@ -146,13 +145,14 @@ def tile_list_lowrank_cross_layer_kernel(
             nc.vector.quantize_mx(out=xq[c, hf][:].bitcast(FP8X4), scales=xs[c, hf][:], in_=woven[:])
 
         hq = [keep.tile([P, HALF], U32, name="hq%d" % hf, align_bytes=64) for hf in range(HALVES)]
-        hs = [keep.tile([P, HALF], U8, name="hs%d" % hf, align_bytes=64) for hf in range(HALVES)]
+        hs = [xs[1, 1][4:, :], keep.tile([P, HALF], U8, name="hs1", align_bytes=64)[:]]
+        h_woven = {}
 
         def project(hf, copy, parts):
             planes = ring.tile([P, PACK, HALF], BF16, name="h_planes")
             woven = ring.tile([P, HALF * PACK], BF16, name="woven", align_bytes=64, bufs=WOVEN_BUFS)
             for t in range(PACK):
-                bank = h_banks[t]
+                bank = h_banks[hf][t]
                 for c in range(PASSES):
                     nc.tensor.matmul_mx(out=bank[:], lhsT=vq[c][:, t * P:(t + 1) * P].bitcast(FP8X4),
                                         lhsT_scale=vs[4 * c:, t * P:(t + 1) * P],
@@ -161,6 +161,10 @@ def tile_list_lowrank_cross_layer_kernel(
                 nc.scalar.activation(out=planes[:, t, :], in_=bank[:], func=COPY, scale=g_sb[:, t:t + 1])
             for cols in parts:
                 weave(copy, woven, planes, cols)
+            h_woven[hf] = woven
+
+        def quantise_h(hf, parts):
+            woven = h_woven[hf]
             for cols in parts:
                 nc.vector.quantize_mx(out=hq[hf][:, cols].bitcast(FP8X4), scales=hs[hf][:, cols],
                                       in_=woven[:, cols.start * PACK:cols.stop * PACK])
@@ -194,7 +198,7 @@ def tile_list_lowrank_cross_layer_kernel(
                                     rhs=xq[c, hf][:].bitcast(FP8X4), rhs_scale=xs[c, hf][:],
                                     start=(c == 0), stop=False)
             nc.tensor.matmul_mx(out=bank[:], lhsT=wdq[i][:].bitcast(FP8X4), lhsT_scale=wds[i][:],
-                                rhs=hq[hf][:].bitcast(FP8X4), rhs_scale=hs[hf][:], start=False, stop=True)
+                                rhs=hq[hf][:].bitcast(FP8X4), rhs_scale=hs[hf], start=False, stop=True)
             cols = slice(hf * HALF, (hf + 1) * HALF)
             nc.vector.scalar_tensor_tensor(out=x0_sb[i][:, cols], in0=bank[:], scalar=b_sb[c_out][:, t:t + 1],
                                            in1=x0_sb[i][:, cols], op0=ADD, op1=MULT)
@@ -205,25 +209,12 @@ def tile_list_lowrank_cross_layer_kernel(
             nc.vector.scalar_tensor_tensor(out=dst, in0=x_raw[c_out][:, hf, t, :], scalar=a_sb[c_out][:, t:t + 1],
                                            in1=dst, op0=MULT, op1=ADD)
 
-        turned = keep.tile([P, HALF], F32, name="turned")
-
-        def add_skip_turned(i, hf):
+        def add_skip_beside(i):
             c_out, t = i // PACK, i % PACK
-            scaled = x_raw[c_out][:, hf, t, :]
-            nc.scalar.activation(out=scaled, in_=scaled, func=COPY, scale=a_sb[c_out][:, t:t + 1])
-            for mb in range(HALF // P):
-                block = slice(mb * P, (mb + 1) * P)
-                nc.tensor.matmul(sum_bank[:, block], lhsT=x0_sb[i][:, hf * HALF + mb * P:hf * HALF + (mb + 1) * P],
-                                 rhs=ident[:], is_transpose=True, start=True, stop=False)
-                nc.tensor.matmul(sum_bank[:, block], lhsT=scaled[:, block], rhs=ident[:],
-                                 is_transpose=True, start=False, stop=True)
-            nc.scalar.copy(out=turned[:], in_=sum_bank[:])
-
-        def turn_back(i, hf):
-            for mb in range(HALF // P):
-                block = slice(mb * P, (mb + 1) * P)
-                nc.tensor.transpose(back_bank[:, block], turned[:, block], ident[:])
-            nc.scalar.copy(out=x0_sb[i][:, hf * HALF:(hf + 1) * HALF], in_=back_bank[:])
+            dst = x0_sb[i][:, HALF:]
+            scaled = x_raw[c_out][:, 0, t, :]
+            nc.scalar.activation(out=scaled, in_=x_raw[c_out][:, 1, t, :], func=COPY, scale=a_sb[c_out][:, t:t + 1])
+            nc.gpsimd.tensor_tensor(out=dst, in0=dst, in1=scaled, op=ADD)
 
         def store(first, count, cols):
             c_out, rows = first // PACK, slice(first % PACK, first % PACK + count)
@@ -239,6 +230,8 @@ def tile_list_lowrank_cross_layer_kernel(
         prepare_x(1, 1, ((on_vector, whole),))
         project(0, on_scalar, (whole,))
         project(1, on_vector, (low, high))
+        quantise_h(0, (whole,))
+        quantise_h(1, (low, high))
         for i in range(WD_AHEAD):
             gather_wd(i)
             turn_wd(i)
@@ -246,7 +239,7 @@ def tile_list_lowrank_cross_layer_kernel(
 
         last = N_TILES - 1
         stores = {3: (0, 4), 5: (4, 2), 6: (6, 1)}
-        by_transposes = range(2, last - 1, 2)
+        beside = range(0, last)
         for i in range(N_TILES):
             ahead = i + WD_AHEAD
             if ahead < N_TILES:
@@ -255,17 +248,17 @@ def tile_list_lowrank_cross_layer_kernel(
             cross(i, 1)
             if ahead < N_TILES:
                 turn_wd(ahead)
-            if i - 1 in by_transposes:
-                turn_back(i - 1, 1)
+            if ahead == last:
+                quantise_wd(ahead)
             add_skip(i, 0)
             if i == last:
                 store(i, 1, slice(0, HALF))
-            if i in by_transposes:
-                add_skip_turned(i, 1)
-            else:
+            if i not in beside:
                 add_skip(i, 1)
-            if ahead < N_TILES:
+            if ahead < last:
                 quantise_wd(ahead)
+            if i in beside:
+                add_skip_beside(i)
             if i in stores:
                 store(*stores[i], slice(0, M))
         store(last, 1, slice(HALF, M))

@@ -28,6 +28,7 @@ N_TILES = N // P
 WD_AHEAD = 1
 RUN = 4
 QUADRANTS = (0, 2, 1, 3)
+ROW0 = 16
 WOVEN_BUFS = 3
 
 
@@ -51,20 +52,26 @@ def tile_list_lowrank_cross_layer_kernel(
         w4s_raw = keep.tile([P, PASSES, N], U8, name="w4s_raw", align_bytes=64)
         tabs_raw = keep.tile([P, T], U8, name="tabs_raw", align_bytes=64)
         tab_raw = [keep.tile([P, T], I32, name="tab_raw%d" % c, align_bytes=64) for c in range(PASSES)]
-        x_raw = [keep.tile([P, HALVES, PACK, HALF], F32, name="x_raw%d" % c) for c in range(PASSES)]
+        x_first = keep.tile([P, PACK, M], F32, name="x_first")
+        x_second = keep.tile([P, HALVES, PACK, HALF], F32, name="x_second")
+
+        def x_raw(c, hf):
+            return x_first[:, :, hf * HALF:(hf + 1) * HALF] if c == 0 else x_second[:, hf]
+
         wd_raw = [keep.tile([P, T], F32, name="wd_raw%d" % i) for i in range(N_TILES)]
         x0_pass = [keep.tile([P, PACK, M], F32, name="x0_pass%d" % c) for c in range(PASSES)]
         x0_sb = [x0_pass[i // PACK][:, i % PACK, :] for i in range(N_TILES)]
-        g_sb = keep.tile([P, PACK], F32, name="g_sb")
-        a_all = keep.tile([P, PASSES, PACK], F32, name="a_all")
-        a_sb = [a_all[:, c, :] for c in range(PASSES)]
-        b_all = keep.tile([P, PASSES, PACK], F32, name="b_all")
-        b_sb = [b_all[:, c, :] for c in range(PASSES)]
+        rows = keep.tile([P, K_PASS], F32, name="rows")
+        columns = keep.tile([P, 2 * PASSES + 1, PACK], F32, name="columns")
+        a_sb = [columns[:, c, :] for c in range(PASSES)]
+        b_sb = [columns[:, PASSES + c, :] for c in range(PASSES)]
+        g_sb = columns[:, 2 * PASSES, :]
         ident = keep.tile([P, P], F32, name="ident")
 
-        nc.vector.memset(w4s_raw[:].rearrange("p c n -> p (c n)").bitcast(I32), 0)
-        nc.gpsimd.memset(tabs_raw[:].bitcast(I32), 0)
+        nc.vector.memset(rows[:], 0.0)
+        nc.vector.memset(tabs_raw[:].bitcast(I32), 0)
         make_identity(nc, ident[:])
+        nc.gpsimd.memset(w4s_raw[:].rearrange("p c n -> p (c n)").bitcast(I32), 0)
 
         x_rows = x.rearrange("(c p t) m -> c p t m", p=P, t=PACK)
         x0_rows = x0.rearrange("(c p t) m -> c p t m", p=P, t=PACK)
@@ -72,7 +79,7 @@ def tile_list_lowrank_cross_layer_kernel(
         wd_rows = wdT.rearrange("(c p t) j -> c t p j", p=P, t=PACK)
 
         def load_x(c, hf):
-            nc.sync.dma_start(out=x_raw[c][:, hf], in_=x_rows[c][:, :, hf * HALF:(hf + 1) * HALF])
+            nc.sync.dma_start(out=x_raw(c, hf), in_=x_rows[c][:, :, hf * HALF:(hf + 1) * HALF])
 
         def load_wd(i):
             nc.sync.dma_start(out=wd_raw[i][:], in_=wd_rows[i // PACK][i % PACK])
@@ -86,20 +93,20 @@ def tile_list_lowrank_cross_layer_kernel(
 
         nc.sync.dma_start(out=w4_raw[:].bitcast(I32), in_=w4_words.rearrange("c p n -> p c n").bitcast(I32))
         nc.sync.dma_start(offsets[:], offs)
-        nc.sync.dma_start(out=g_sb[:], in_=g.rearrange("(p t) -> p t", t=PACK))
-        nc.sync.dma_start(out=a_all[:], in_=a.rearrange("(c p t) -> p c t", p=P, t=PACK))
-        nc.sync.dma_start(out=b_all[:], in_=b.rearrange("(c p t) -> p c t", p=P, t=PACK))
-        load_x(0, 0)
+        for r, vector in enumerate((a, b, g)):
+            row = ROW0 + PASSES * r
+            nc.sync.dma_start(out=rows[row:row + vector.shape[0] // K_PASS, :],
+                              in_=vector.rearrange("(c n) -> c n", n=K_PASS))
+        nc.sync.dma_start(out=x_first[:], in_=x_rows[0])
+        for q in QUADRANTS:
+            nc.sync.dma_start(out=tabs_raw[32 * q + 4:32 * q + 12, :].bitcast(I32),
+                              in_=tab_scales[:, 4 * q:4 * q + 4, :].bitcast(I32))
         load_tab(0)
         load_tab(1)
-        for q in QUADRANTS:
-            nc.sync.dma_start(out=tabs_raw[32 * q:32 * q + 8, :].bitcast(I32),
-                              in_=tab_scales[:, 4 * q:4 * q + 4, :].bitcast(I32))
         load_x(1, 0)
         for q in QUADRANTS:
             nc.sync.dma_start(out=w4s_raw[32 * q:32 * q + 4].bitcast(I32),
                               in_=w4_scales[:, 4 * q:4 * q + 4, :].rearrange("c r n -> r c n").bitcast(I32))
-        load_x(0, 1)
         load_x(1, 1)
         for i in range(WD_AHEAD):
             load_wd(i)
@@ -115,15 +122,20 @@ def tile_list_lowrank_cross_layer_kernel(
                 out=w4q[:, c, :].bitcast(U16).rearrange("p (d t q) -> p d t q", t=PACK, q=P),
                 in_=w4_raw[:, c, :].bitcast(U16).rearrange("p (d q t) -> p d t q", t=PACK, q=P))
 
+        for t in range(PACK):
+            nc.tensor.transpose(banks[0][:, t * P:(t + 1) * P], rows[:, t:K_PASS:PACK], ident[:])
+        nc.scalar.copy(out=columns[:],
+                       in_=banks[0][:].rearrange("p (t k) -> p k t", t=PACK)[:, ROW0:ROW0 + 2 * PASSES + 1, :])
+
         vq = [keep.tile([P, S], U32, name="vq%d" % c, align_bytes=64) for c in range(PASSES)]
         vs_listed = keep.tile([P, S], U8, name="vs_listed", align_bytes=64)
         vs = keep.tile([P, S], U8, name="vs", align_bytes=64)
-        for c in range(PASSES):
-            nc.vector.tensor_copy(out=vq[c][:].rearrange("p (t q) -> p q t", t=PACK),
-                                  in_=tab_raw[c][:].bitcast(U32).indirect(offsets[:]))
         nc.vector.tensor_copy(out=vs_listed[:], in_=tabs_raw[:].indirect(offsets[:]))
         nc.vector.tensor_copy(out=vs[:].rearrange("p (t q) -> p t q", t=PACK),
                               in_=vs_listed[:].rearrange("p (q t) -> p t q", t=PACK))
+        for c in range(PASSES):
+            nc.vector.tensor_copy(out=vq[c][:].rearrange("p (t q) -> p q t", t=PACK),
+                                  in_=tab_raw[c][:].bitcast(U32).indirect(offsets[:]))
 
         xq = {}
         xs = {}
@@ -141,21 +153,21 @@ def tile_list_lowrank_cross_layer_kernel(
         def prepare_x(c, hf, shares):
             woven = ring.tile([P, HALF * PACK], BF16, name="woven", align_bytes=64, bufs=WOVEN_BUFS)
             for copy, cols in shares:
-                weave(copy, woven, x_raw[c][:, hf], cols)
+                weave(copy, woven, x_raw(c, hf), cols)
             nc.vector.quantize_mx(out=xq[c, hf][:].bitcast(FP8X4), scales=xs[c, hf][:], in_=woven[:])
+            return woven
 
         hq = [keep.tile([P, HALF], U32, name="hq%d" % hf, align_bytes=64) for hf in range(HALVES)]
         hs = [xs[1, 1][4:, :], keep.tile([P, HALF], U8, name="hs1", align_bytes=64)[:]]
         h_woven = {}
 
-        def project(hf, copy, parts):
+        def project(hf, copy, parts, woven):
             planes = ring.tile([P, PACK, HALF], BF16, name="h_planes")
-            woven = ring.tile([P, HALF * PACK], BF16, name="woven", align_bytes=64, bufs=WOVEN_BUFS)
             for t in range(PACK):
                 bank = h_banks[hf][t]
                 for c in range(PASSES):
                     nc.tensor.matmul_mx(out=bank[:], lhsT=vq[c][:, t * P:(t + 1) * P].bitcast(FP8X4),
-                                        lhsT_scale=vs[4 * c:, t * P:(t + 1) * P],
+                                        lhsT_scale=vs[4 * (c + 1):, t * P:(t + 1) * P],
                                         rhs=xq[c, hf][:].bitcast(FP8X4), rhs_scale=xs[c, hf][:],
                                         start=(c == 0), stop=(c == PASSES - 1))
                 nc.scalar.activation(out=planes[:, t, :], in_=bank[:], func=COPY, scale=g_sb[:, t:t + 1])
@@ -206,14 +218,14 @@ def tile_list_lowrank_cross_layer_kernel(
         def add_skip(i, hf):
             c_out, t = i // PACK, i % PACK
             dst = x0_sb[i][:, hf * HALF:(hf + 1) * HALF]
-            nc.vector.scalar_tensor_tensor(out=dst, in0=x_raw[c_out][:, hf, t, :], scalar=a_sb[c_out][:, t:t + 1],
+            nc.vector.scalar_tensor_tensor(out=dst, in0=x_raw(c_out, hf)[:, t, :], scalar=a_sb[c_out][:, t:t + 1],
                                            in1=dst, op0=MULT, op1=ADD)
 
         def add_skip_beside(i):
             c_out, t = i // PACK, i % PACK
             dst = x0_sb[i][:, HALF:]
-            scaled = x_raw[c_out][:, 0, t, :]
-            nc.scalar.activation(out=scaled, in_=x_raw[c_out][:, 1, t, :], func=COPY, scale=a_sb[c_out][:, t:t + 1])
+            scaled = x_raw(c_out, 0)[:, t, :]
+            nc.scalar.activation(out=scaled, in_=x_raw(c_out, 1)[:, t, :], func=COPY, scale=a_sb[c_out][:, t:t + 1])
             nc.gpsimd.tensor_tensor(out=dst, in0=dst, in1=scaled, op=ADD)
 
         def store(first, count, cols):
@@ -222,14 +234,14 @@ def tile_list_lowrank_cross_layer_kernel(
 
         on_vector, on_scalar = nc.vector.tensor_copy, nc.scalar.copy
         prepare_x(0, 0, ((on_scalar, whole),))
-        prepare_x(1, 0, ((on_vector, low), (on_scalar, high)))
+        prepare_x(0, 1, ((on_scalar, whole),))
+        spent_first = prepare_x(1, 0, ((on_vector, low), (on_scalar, high)))
         nc.vector.tensor_copy(
             out=w4s[:].rearrange("p c (d t q) -> p (c d) t q", t=PACK, q=P),
             in_=w4s_raw[:].rearrange("p c (d q t) -> p (c d) t q", t=PACK, q=P))
-        prepare_x(0, 1, ((on_vector, whole),))
-        prepare_x(1, 1, ((on_vector, whole),))
-        project(0, on_scalar, (whole,))
-        project(1, on_vector, (low, high))
+        spent_last = prepare_x(1, 1, ((on_vector, whole),))
+        project(0, on_vector, (whole,), spent_last)
+        project(1, on_vector, (low, high), spent_first)
         quantise_h(0, (whole,))
         quantise_h(1, (low, high))
         for i in range(WD_AHEAD):
@@ -239,7 +251,7 @@ def tile_list_lowrank_cross_layer_kernel(
 
         last = N_TILES - 1
         stores = {3: (0, 4), 5: (4, 2), 6: (6, 1)}
-        beside = range(0, last)
+        beside = range(0, last - 1)
         for i in range(N_TILES):
             ahead = i + WD_AHEAD
             if ahead < N_TILES:

@@ -48,9 +48,11 @@ def tile_list_lowrank_cross_layer_kernel(
             return banks[2 * (i % 2) + hf]
 
         offsets = keep.tile([P, S // 16], U16, name="offsets")
-        w4_raw = keep.tile([P, PASSES, 2 * N], U8, name="w4_raw", align_bytes=64)
+        w4_raw = [keep.tile([P, 2 * N], U8, name="w4_raw%d" % c, align_bytes=64) for c in range(PASSES)]
         w4s_raw = keep.tile([P, PASSES, N], U8, name="w4s_raw", align_bytes=64)
         tabs_raw = keep.tile([P, T], U8, name="tabs_raw", align_bytes=64)
+        vs = keep.tile([P, PASSES, S], U8, name="vs", align_bytes=64)
+        vs_words = vs[:].rearrange("p c s -> p (c s)").bitcast(I32)
         tab_raw = [keep.tile([P, T], I32, name="tab_raw%d" % c, align_bytes=64) for c in range(PASSES)]
         x_first = keep.tile([P, PACK, M], F32, name="x_first")
         x_second = keep.tile([P, HALVES, PACK, HALF], F32, name="x_second")
@@ -68,10 +70,11 @@ def tile_list_lowrank_cross_layer_kernel(
         g_sb = columns[:, 2 * PASSES, :]
         ident = keep.tile([P, P], F32, name="ident")
 
+        nc.gpsimd.memset(tabs_raw[:].bitcast(I32), 0)
         nc.vector.memset(rows[:], 0.0)
-        nc.vector.memset(tabs_raw[:].bitcast(I32), 0)
-        make_identity(nc, ident[:])
         nc.gpsimd.memset(w4s_raw[:].rearrange("p c n -> p (c n)").bitcast(I32), 0)
+        make_identity(nc, ident[:])
+        nc.gpsimd.memset(vs_words, 0)
 
         x_rows = x.rearrange("(c p t) m -> c p t m", p=P, t=PACK)
         x0_rows = x0.rearrange("(c p t) m -> c p t m", p=P, t=PACK)
@@ -91,22 +94,37 @@ def tile_list_lowrank_cross_layer_kernel(
         def load_tab(c):
             nc.sync.dma_start(out=tab_raw[c][:], in_=tab_words[c].rearrange("p n t -> p (n t)").bitcast(I32))
 
-        nc.sync.dma_start(out=w4_raw[:].bitcast(I32), in_=w4_words.rearrange("c p n -> p c n").bitcast(I32))
+        def load_w4(c):
+            nc.sync.dma_start(out=w4_raw[c][:].bitcast(I32), in_=w4_words[c].bitcast(I32))
+
+        def load_w4_scales(q):
+            nc.sync.dma_start(out=w4s_raw[32 * q:32 * q + 4].bitcast(I32),
+                              in_=w4_scales[:, 4 * q:4 * q + 4, :].rearrange("c r n -> r c n").bitcast(I32))
+
+        load_w4(0)
         nc.sync.dma_start(offsets[:], offs)
+        nc.sync.dma_start(out=tabs_raw[0:P:4].bitcast(I32), in_=tab_scales.rearrange("c z n -> z c n").bitcast(I32))
+        nc.sync.dma_start(out=x_first[:], in_=x_rows[0])
         for r, vector in enumerate((a, b, g)):
             row = ROW0 + PASSES * r
             nc.sync.dma_start(out=rows[row:row + vector.shape[0] // K_PASS, :],
                               in_=vector.rearrange("(c n) -> c n", n=K_PASS))
-        nc.sync.dma_start(out=x_first[:], in_=x_rows[0])
-        for q in QUADRANTS:
-            nc.sync.dma_start(out=tabs_raw[32 * q + 4:32 * q + 12, :].bitcast(I32),
-                              in_=tab_scales[:, 4 * q:4 * q + 4, :].bitcast(I32))
+        load_w4_scales(QUADRANTS[0])
         load_tab(0)
         load_tab(1)
-        load_x(1, 0)
+        load_w4_scales(QUADRANTS[1])
+        vs_listed = keep.tile([P, S], U8, name="vs_listed", align_bytes=64)
+        vs_dealt = keep.tile([P, S], U8, name="vs_dealt", align_bytes=64)
+        nc.vector.tensor_copy(out=vs_listed[:], in_=tabs_raw[:].indirect(offsets[:]))
+        nc.vector.tensor_copy(out=vs_dealt[:].rearrange("p (t q) -> p t q", t=PACK),
+                              in_=vs_listed[:].rearrange("p (q t) -> p t q", t=PACK))
         for q in QUADRANTS:
-            nc.sync.dma_start(out=w4s_raw[32 * q:32 * q + 4].bitcast(I32),
-                              in_=w4_scales[:, 4 * q:4 * q + 4, :].rearrange("c r n -> r c n").bitcast(I32))
+            nc.sync.dma_start(out=vs[32 * q + 4:32 * q + 8].bitcast(I32),
+                              in_=vs_dealt[32 * q:32 * q + 32:4].bitcast(I32))
+        load_w4(1)
+        load_x(1, 0)
+        load_w4_scales(QUADRANTS[2])
+        load_w4_scales(QUADRANTS[3])
         load_x(1, 1)
         for i in range(WD_AHEAD):
             load_wd(i)
@@ -120,7 +138,7 @@ def tile_list_lowrank_cross_layer_kernel(
         for c in range(PASSES):
             nc.vector.tensor_copy(
                 out=w4q[:, c, :].bitcast(U16).rearrange("p (d t q) -> p d t q", t=PACK, q=P),
-                in_=w4_raw[:, c, :].bitcast(U16).rearrange("p (d q t) -> p d t q", t=PACK, q=P))
+                in_=w4_raw[c][:].bitcast(U16).rearrange("p (d q t) -> p d t q", t=PACK, q=P))
 
         for t in range(PACK):
             nc.tensor.transpose(banks[0][:, t * P:(t + 1) * P], rows[:, t:K_PASS:PACK], ident[:])
@@ -128,11 +146,6 @@ def tile_list_lowrank_cross_layer_kernel(
                        in_=banks[0][:].rearrange("p (t k) -> p k t", t=PACK)[:, ROW0:ROW0 + 2 * PASSES + 1, :])
 
         vq = [keep.tile([P, S], U32, name="vq%d" % c, align_bytes=64) for c in range(PASSES)]
-        vs_listed = keep.tile([P, S], U8, name="vs_listed", align_bytes=64)
-        vs = keep.tile([P, S], U8, name="vs", align_bytes=64)
-        nc.vector.tensor_copy(out=vs_listed[:], in_=tabs_raw[:].indirect(offsets[:]))
-        nc.vector.tensor_copy(out=vs[:].rearrange("p (t q) -> p t q", t=PACK),
-                              in_=vs_listed[:].rearrange("p (q t) -> p t q", t=PACK))
         for c in range(PASSES):
             nc.vector.tensor_copy(out=vq[c][:].rearrange("p (t q) -> p q t", t=PACK),
                                   in_=tab_raw[c][:].bitcast(U32).indirect(offsets[:]))
@@ -167,7 +180,7 @@ def tile_list_lowrank_cross_layer_kernel(
                 bank = h_banks[hf][t]
                 for c in range(PASSES):
                     nc.tensor.matmul_mx(out=bank[:], lhsT=vq[c][:, t * P:(t + 1) * P].bitcast(FP8X4),
-                                        lhsT_scale=vs[4 * (c + 1):, t * P:(t + 1) * P],
+                                        lhsT_scale=vs[4:, c, t * P:(t + 1) * P],
                                         rhs=xq[c, hf][:].bitcast(FP8X4), rhs_scale=xs[c, hf][:],
                                         start=(c == 0), stop=(c == PASSES - 1))
                 nc.scalar.activation(out=planes[:, t, :], in_=bank[:], func=COPY, scale=g_sb[:, t:t + 1])

@@ -27,6 +27,8 @@ HALVES = M // HALF
 N_TILES = N // P
 WD_AHEAD = 1
 RUN = 4
+QUADRANT = 32
+LIVE = 4
 QUADRANTS = (0, 2, 1, 3)
 ROW0 = 16
 WOVEN_BUFS = 3
@@ -48,7 +50,7 @@ def tile_list_lowrank_cross_layer_kernel(
             return banks[2 * (i % 2) + hf]
 
         offsets = keep.tile([P, S // 16], U16, name="offsets")
-        w4_raw = [keep.tile([P, 2 * N], U8, name="w4_raw%d" % c, align_bytes=64) for c in range(PASSES)]
+        w4_raw = keep.tile([P, PASSES, 2 * N], U8, name="w4_raw", align_bytes=64)
         w4s_raw = keep.tile([P, PASSES, N], U8, name="w4s_raw", align_bytes=64)
         tabs_raw = keep.tile([P, T], U8, name="tabs_raw", align_bytes=64)
         vs = keep.tile([P, PASSES, S], U8, name="vs", align_bytes=64)
@@ -63,16 +65,18 @@ def tile_list_lowrank_cross_layer_kernel(
         wd_raw = [keep.tile([P, T], F32, name="wd_raw%d" % i) for i in range(N_TILES)]
         x0_pass = [keep.tile([P, PACK, M], F32, name="x0_pass%d" % c) for c in range(PASSES)]
         x0_sb = [x0_pass[i // PACK][:, i % PACK, :] for i in range(N_TILES)]
-        rows = keep.tile([P, K_PASS], F32, name="rows")
-        columns = keep.tile([P, 2 * PASSES + 1, PACK], F32, name="columns")
-        a_sb = [columns[:, c, :] for c in range(PASSES)]
-        b_sb = [columns[:, PASSES + c, :] for c in range(PASSES)]
-        g_sb = columns[:, 2 * PASSES, :]
+        ab_rows = keep.tile([P, K_PASS], F32, name="rows")
+        g_row = keep.tile([P, K_PASS], F32, name="g_row")
+        ab_sb = keep.tile([P, 2 * PASSES, PACK], F32, name="columns")
+        g_sb = keep.tile([P, 1, PACK], F32, name="g_sb")
+        a_sb = [ab_sb[:, c, :] for c in range(PASSES)]
+        b_sb = [ab_sb[:, PASSES + c, :] for c in range(PASSES)]
         ident = keep.tile([P, P], F32, name="ident")
 
         nc.gpsimd.memset(tabs_raw[:].bitcast(I32), 0)
-        nc.vector.memset(rows[:], 0.0)
-        nc.gpsimd.memset(w4s_raw[:].rearrange("p c n -> p (c n)").bitcast(I32), 0)
+        nc.vector.memset(w4s_raw[:].rearrange("p c n -> p (c n)").bitcast(I32), 0)
+        nc.vector.memset(g_row[:], 0.0)
+        nc.vector.memset(ab_rows[:], 0.0)
         make_identity(nc, ident[:])
         nc.gpsimd.memset(vs_words, 0)
 
@@ -88,44 +92,43 @@ def tile_list_lowrank_cross_layer_kernel(
             nc.sync.dma_start(out=wd_raw[i][:], in_=wd_rows[i // PACK][i % PACK])
 
         def load_x0(first, count):
-            rows = slice(first % PACK, first % PACK + count)
-            nc.sync.dma_start(out=x0_pass[first // PACK][:, rows, :], in_=x0_rows[first // PACK][:, rows, :])
+            slots = slice(first % PACK, first % PACK + count)
+            nc.sync.dma_start(out=x0_pass[first // PACK][:, slots, :], in_=x0_rows[first // PACK][:, slots, :])
 
         def load_tab(c):
             nc.sync.dma_start(out=tab_raw[c][:], in_=tab_words[c].rearrange("p n t -> p (n t)").bitcast(I32))
 
-        def load_w4(c):
-            nc.sync.dma_start(out=w4_raw[c][:].bitcast(I32), in_=w4_words[c].bitcast(I32))
+        def load_rows(tile, vector, row):
+            nc.sync.dma_start(out=tile[row:row + vector.shape[0] // K_PASS, :],
+                              in_=vector.rearrange("(c n) -> c n", n=K_PASS))
 
         def load_w4_scales(q):
-            nc.sync.dma_start(out=w4s_raw[32 * q:32 * q + 4].bitcast(I32),
-                              in_=w4_scales[:, 4 * q:4 * q + 4, :].rearrange("c r n -> r c n").bitcast(I32))
+            nc.sync.dma_start(out=w4s_raw[QUADRANT * q:QUADRANT * q + LIVE].bitcast(I32),
+                              in_=w4_scales[:, LIVE * q:LIVE * (q + 1), :].rearrange("c r n -> r c n").bitcast(I32))
 
-        load_w4(0)
+        nc.sync.dma_start(out=w4_raw[:].bitcast(I32), in_=w4_words.rearrange("c p n -> p c n").bitcast(I32))
         nc.sync.dma_start(offsets[:], offs)
-        nc.sync.dma_start(out=tabs_raw[0:P:4].bitcast(I32), in_=tab_scales.rearrange("c z n -> z c n").bitcast(I32))
+        nc.sync.dma_start(out=tabs_raw[0:P:LIVE].bitcast(I32),
+                          in_=tab_scales.rearrange("c z n -> z c n").bitcast(I32))
         nc.sync.dma_start(out=x_first[:], in_=x_rows[0])
-        for r, vector in enumerate((a, b, g)):
-            row = ROW0 + PASSES * r
-            nc.sync.dma_start(out=rows[row:row + vector.shape[0] // K_PASS, :],
-                              in_=vector.rearrange("(c n) -> c n", n=K_PASS))
-        load_w4_scales(QUADRANTS[0])
+        load_rows(g_row, g, ROW0)
+        for q in QUADRANTS[:-1]:
+            load_w4_scales(q)
         load_tab(0)
         load_tab(1)
-        load_w4_scales(QUADRANTS[1])
+        load_w4_scales(QUADRANTS[-1])
         vs_listed = keep.tile([P, S], U8, name="vs_listed", align_bytes=64)
         vs_dealt = keep.tile([P, S], U8, name="vs_dealt", align_bytes=64)
         nc.vector.tensor_copy(out=vs_listed[:], in_=tabs_raw[:].indirect(offsets[:]))
         nc.vector.tensor_copy(out=vs_dealt[:].rearrange("p (t q) -> p t q", t=PACK),
                               in_=vs_listed[:].rearrange("p (q t) -> p t q", t=PACK))
         for q in QUADRANTS:
-            nc.sync.dma_start(out=vs[32 * q + 4:32 * q + 8].bitcast(I32),
-                              in_=vs_dealt[32 * q:32 * q + 32:4].bitcast(I32))
-        load_w4(1)
+            nc.sync.dma_start(out=vs[QUADRANT * q + LIVE:QUADRANT * q + 2 * LIVE].bitcast(I32),
+                              in_=vs_dealt[QUADRANT * q:QUADRANT * (q + 1):LIVE].bitcast(I32))
         load_x(1, 0)
-        load_w4_scales(QUADRANTS[2])
-        load_w4_scales(QUADRANTS[3])
         load_x(1, 1)
+        load_rows(ab_rows, a, ROW0)
+        load_rows(ab_rows, b, ROW0 + PASSES)
         for i in range(WD_AHEAD):
             load_wd(i)
         for i in range(N_TILES - WD_AHEAD):
@@ -138,12 +141,15 @@ def tile_list_lowrank_cross_layer_kernel(
         for c in range(PASSES):
             nc.vector.tensor_copy(
                 out=w4q[:, c, :].bitcast(U16).rearrange("p (d t q) -> p d t q", t=PACK, q=P),
-                in_=w4_raw[c][:].bitcast(U16).rearrange("p (d q t) -> p d t q", t=PACK, q=P))
+                in_=w4_raw[:, c, :].bitcast(U16).rearrange("p (d q t) -> p d t q", t=PACK, q=P))
 
-        for t in range(PACK):
-            nc.tensor.transpose(banks[0][:, t * P:(t + 1) * P], rows[:, t:K_PASS:PACK], ident[:])
-        nc.scalar.copy(out=columns[:],
-                       in_=banks[0][:].rearrange("p (t k) -> p k t", t=PACK)[:, ROW0:ROW0 + 2 * PASSES + 1, :])
+        def turn_rows(dst, src, bank):
+            for t in range(PACK):
+                nc.tensor.transpose(bank[:, t * P:(t + 1) * P], src[:, t:K_PASS:PACK], ident[:])
+            nc.scalar.copy(out=dst[:],
+                           in_=bank[:].rearrange("p (t r) -> p r t", t=PACK)[:, ROW0:ROW0 + dst.shape[1], :])
+
+        turn_rows(g_sb, g_row, h_banks[1][0])
 
         vq = [keep.tile([P, S], U32, name="vq%d" % c, align_bytes=64) for c in range(PASSES)]
         for c in range(PASSES):
@@ -159,9 +165,9 @@ def tile_list_lowrank_cross_layer_kernel(
 
         low, high, whole = slice(0, HALF // 2), slice(HALF // 2, HALF), slice(0, HALF)
 
-        def weave(copy, woven, rows, cols):
+        def weave(copy, woven, by_slot, cols):
             copy(out=woven[:, cols.start * PACK:cols.stop * PACK].rearrange("p (m i t) -> p m t i", i=RUN, t=PACK),
-                 in_=rows[:, :, cols].rearrange("p t (m i) -> p m t i", i=RUN))
+                 in_=by_slot[:, :, cols].rearrange("p t (m i) -> p m t i", i=RUN))
 
         def prepare_x(c, hf, shares):
             woven = ring.tile([P, HALF * PACK], BF16, name="woven", align_bytes=64, bufs=WOVEN_BUFS)
@@ -171,21 +177,21 @@ def tile_list_lowrank_cross_layer_kernel(
             return woven
 
         hq = [keep.tile([P, HALF], U32, name="hq%d" % hf, align_bytes=64) for hf in range(HALVES)]
-        hs = [xs[1, 1][4:, :], keep.tile([P, HALF], U8, name="hs1", align_bytes=64)[:]]
+        hs = [xs[1, 1][LIVE:, :], keep.tile([P, HALF], U8, name="hs1", align_bytes=64)[:]]
         h_woven = {}
 
-        def project(hf, copy, parts, woven):
-            planes = ring.tile([P, PACK, HALF], BF16, name="h_planes")
+        def project(hf, shares, woven):
+            by_slot = ring.tile([P, PACK, HALF], BF16, name="h_planes")
             for t in range(PACK):
                 bank = h_banks[hf][t]
                 for c in range(PASSES):
                     nc.tensor.matmul_mx(out=bank[:], lhsT=vq[c][:, t * P:(t + 1) * P].bitcast(FP8X4),
-                                        lhsT_scale=vs[4:, c, t * P:(t + 1) * P],
+                                        lhsT_scale=vs[LIVE:, c, t * P:(t + 1) * P],
                                         rhs=xq[c, hf][:].bitcast(FP8X4), rhs_scale=xs[c, hf][:],
                                         start=(c == 0), stop=(c == PASSES - 1))
-                nc.scalar.activation(out=planes[:, t, :], in_=bank[:], func=COPY, scale=g_sb[:, t:t + 1])
-            for cols in parts:
-                weave(copy, woven, planes, cols)
+                nc.scalar.activation(out=by_slot[:, t, :], in_=bank[:], func=COPY, scale=g_sb[:, 0, t:t + 1])
+            for copy, cols in shares:
+                weave(copy, woven, by_slot, cols)
             h_woven[hf] = woven
 
         def quantise_h(hf, parts):
@@ -242,19 +248,20 @@ def tile_list_lowrank_cross_layer_kernel(
             nc.gpsimd.tensor_tensor(out=dst, in0=dst, in1=scaled, op=ADD)
 
         def store(first, count, cols):
-            c_out, rows = first // PACK, slice(first % PACK, first % PACK + count)
-            nc.sync.dma_start(out=out_rows[c_out][:, rows, cols], in_=x0_pass[c_out][:, rows, cols])
+            c_out, slots = first // PACK, slice(first % PACK, first % PACK + count)
+            nc.sync.dma_start(out=out_rows[c_out][:, slots, cols], in_=x0_pass[c_out][:, slots, cols])
 
         on_vector, on_scalar = nc.vector.tensor_copy, nc.scalar.copy
         prepare_x(0, 0, ((on_scalar, whole),))
         prepare_x(0, 1, ((on_scalar, whole),))
-        spent_first = prepare_x(1, 0, ((on_vector, low), (on_scalar, high)))
         nc.vector.tensor_copy(
             out=w4s[:].rearrange("p c (d t q) -> p (c d) t q", t=PACK, q=P),
             in_=w4s_raw[:].rearrange("p c (d q t) -> p (c d) t q", t=PACK, q=P))
+        spent_first = prepare_x(1, 0, ((on_vector, low), (on_scalar, high)))
         spent_last = prepare_x(1, 1, ((on_vector, whole),))
-        project(0, on_vector, (whole,), spent_last)
-        project(1, on_vector, (low, high), spent_first)
+        project(0, ((on_vector, whole),), spent_last)
+        project(1, ((on_vector, low), (on_scalar, high)), spent_first)
+        turn_rows(ab_sb, ab_rows, h_banks[0][0])
         quantise_h(0, (whole,))
         quantise_h(1, (low, high))
         for i in range(WD_AHEAD):

@@ -64,7 +64,10 @@ def tile_list_lowrank_cross_layer_kernel(
 
         wd_raw = [keep.tile([P, T], F32, name="wd_raw%d" % i) for i in range(N_TILES)]
         x0_pass = [keep.tile([P, PACK, M], F32, name="x0_pass%d" % c) for c in range(PASSES)]
-        x0_sb = [x0_pass[i // PACK][:, i % PACK, :] for i in range(N_TILES)]
+        x0_sb = [x0_pass[i // PACK][:, i % PACK, :] for i in range(N_TILES - 2)]
+        x0_last = keep.tile([P, 2 * M], F32, name="x0_last", align_bytes=64)
+        x0_sb.extend((x0_last[:, :M], x0_last[:, M:]))
+        res_sb = [x0_pass[i // PACK][:, i % PACK, :] for i in range(N_TILES)]
         ab_rows = keep.tile([P, K_PASS], F32, name="rows")
         g_row = keep.tile([P, K_PASS], F32, name="g_row")
         ab_sb = keep.tile([P, 2 * PASSES, PACK], F32, name="columns")
@@ -103,8 +106,8 @@ def tile_list_lowrank_cross_layer_kernel(
                               in_=vector.rearrange("(c n) -> c n", n=K_PASS))
 
         def load_w4_scales(q):
-            nc.sync.dma_start(out=w4s_raw[QUADRANT * q:QUADRANT * q + LIVE].bitcast(I32),
-                              in_=w4_scales[:, LIVE * q:LIVE * (q + 1), :].rearrange("c r n -> r c n").bitcast(I32))
+            nc.sync.dma_start(out=w4s_raw[q:P:QUADRANT].bitcast(I32),
+                              in_=w4_scales[:, q:16:LIVE, :].rearrange("c r n -> r c n").bitcast(I32))
 
         nc.sync.dma_start(out=w4_raw[:].bitcast(I32), in_=w4_words.rearrange("c p n -> p c n").bitcast(I32))
         nc.sync.dma_start(offsets[:], offs)
@@ -131,10 +134,11 @@ def tile_list_lowrank_cross_layer_kernel(
         load_rows(ab_rows, b, ROW0 + PASSES)
         for i in range(WD_AHEAD):
             load_wd(i)
-        for i in range(N_TILES - WD_AHEAD):
+        for i in range(N_TILES - 2):
             load_wd(i + WD_AHEAD)
             load_x0(i, 1)
-        load_x0(N_TILES - WD_AHEAD, WD_AHEAD)
+        load_wd(N_TILES - 1)
+        nc.sync.dma_start(out=x0_last[:].rearrange("p (t m) -> p t m", t=2), in_=x0_rows[1][:, 2:4, :])
 
         w4q = keep.tile([P, PASSES, 2 * N], U8, name="w4q", align_bytes=64)
         w4s = keep.tile([P, PASSES, N], U8, name="w4s", align_bytes=64)
@@ -213,12 +217,15 @@ def tile_list_lowrank_cross_layer_kernel(
             bank = wd_banks[i % 2][:, :2 * P].rearrange("p (u n) -> p u n", u=2)
             for u in range(2):
                 nc.tensor.transpose(bank[:, u, :], pairs[:, u:S // 2:2], ident[:])
-            wd_woven[i] = ring.tile([P, P * PACK], BF16, name="wd_woven", align_bytes=64)
-            nc.scalar.copy(out=wd_woven[i][:].bitcast(F32).rearrange("p (n u) -> p n u", u=2),
-                           in_=bank.rearrange("p u n -> p n u"))
+            if i < N_TILES - 1:
+                words = ring.tile([P, 2 * P], F32, name="wd_woven", align_bytes=64)[:]
+            else:
+                words = x0_sb[i - 1][:, :2 * P]
+            wd_woven[i] = words.bitcast(BF16)
+            nc.scalar.copy(out=words.rearrange("p (n u) -> p n u", u=2), in_=bank.rearrange("p u n -> p n u"))
 
         def quantise_wd(i):
-            nc.vector.quantize_mx(out=wdq[i][:].bitcast(FP8X4), scales=wds[i][:], in_=wd_woven[i][:])
+            nc.vector.quantize_mx(out=wdq[i][:].bitcast(FP8X4), scales=wds[i][:], in_=wd_woven[i])
 
         def cross(i, hf):
             c_out, t = i // PACK, i % PACK
@@ -231,18 +238,18 @@ def tile_list_lowrank_cross_layer_kernel(
             nc.tensor.matmul_mx(out=bank[:], lhsT=wdq[i][:].bitcast(FP8X4), lhsT_scale=wds[i][:],
                                 rhs=hq[hf][:].bitcast(FP8X4), rhs_scale=hs[hf], start=False, stop=True)
             cols = slice(hf * HALF, (hf + 1) * HALF)
-            nc.vector.scalar_tensor_tensor(out=x0_sb[i][:, cols], in0=bank[:], scalar=b_sb[c_out][:, t:t + 1],
+            nc.vector.scalar_tensor_tensor(out=res_sb[i][:, cols], in0=bank[:], scalar=b_sb[c_out][:, t:t + 1],
                                            in1=x0_sb[i][:, cols], op0=ADD, op1=MULT)
 
         def add_skip(i, hf):
             c_out, t = i // PACK, i % PACK
-            dst = x0_sb[i][:, hf * HALF:(hf + 1) * HALF]
+            dst = res_sb[i][:, hf * HALF:(hf + 1) * HALF]
             nc.vector.scalar_tensor_tensor(out=dst, in0=x_raw(c_out, hf)[:, t, :], scalar=a_sb[c_out][:, t:t + 1],
                                            in1=dst, op0=MULT, op1=ADD)
 
         def add_skip_beside(i):
             c_out, t = i // PACK, i % PACK
-            dst = x0_sb[i][:, HALF:]
+            dst = res_sb[i][:, HALF:]
             scaled = x_raw(c_out, 0)[:, t, :]
             nc.scalar.activation(out=scaled, in_=x_raw(c_out, 1)[:, t, :], func=COPY, scale=a_sb[c_out][:, t:t + 1])
             nc.gpsimd.tensor_tensor(out=dst, in0=dst, in1=scaled, op=ADD)

@@ -25,13 +25,15 @@ PASSES = K // K_PASS
 HALF = 512
 HALVES = M // HALF
 N_TILES = N // P
-WD_AHEAD = 1
 RUN = 4
 QUADRANT = 32
 LIVE = 4
 QUADRANTS = (0, 2, 1, 3)
 ROW0 = 16
+ROW_STEP = 64
 WOVEN_BUFS = 3
+X0_PAIRS = 3
+VECTOR_SHARE = 352
 
 
 def tile_list_lowrank_cross_layer_kernel(
@@ -43,53 +45,42 @@ def tile_list_lowrank_cross_layer_kernel(
         ring = ctx.enter_context(tc.tile_pool(name="ring", bufs=2))
         psum = ctx.enter_context(tc.psum_pool(name="psum", bufs=1))
         banks = [psum.tile([P, HALF], F32, name="bank%d" % k) for k in range(8)]
-        h_banks = (banks[4:], banks[:4])
-        wd_banks = banks[6:]
+        h_banks = (banks[:2] + banks[6:], banks[2:6])
 
         def y_bank(i, hf):
-            return banks[2 * (i % 2) + hf]
+            return banks[2 * (i % 3) + hf]
+
+        def wd_bank(i):
+            if i % 2 == 1 and i < 2 * X0_PAIRS:
+                return y_bank(i - 1, 0)
+            return banks[6]
 
         offsets = keep.tile([P, S // 16], U16, name="offsets")
+        tabs_raw = keep.tile([P, T], U8, name="tabs_raw", align_bytes=64)
+        tab_raw = [keep.tile([P, T], I32, name="tab_raw%d" % c, align_bytes=64) for c in range(PASSES)]
         w4_raw = keep.tile([P, PASSES, 2 * N], U8, name="w4_raw", align_bytes=64)
         w4s_raw = keep.tile([P, PASSES, N], U8, name="w4s_raw", align_bytes=64)
-        tabs_raw = keep.tile([P, T], U8, name="tabs_raw", align_bytes=64)
         vs = keep.tile([P, PASSES, S], U8, name="vs", align_bytes=64)
-        vs_words = vs[:].rearrange("p c s -> p (c s)").bitcast(I32)
-        tab_raw = [keep.tile([P, T], I32, name="tab_raw%d" % c, align_bytes=64) for c in range(PASSES)]
-        x_first = keep.tile([P, PACK, M], F32, name="x_first")
-        x_second = keep.tile([P, HALVES, PACK, HALF], F32, name="x_second")
-
-        def x_raw(c, hf):
-            return x_first[:, :, hf * HALF:(hf + 1) * HALF] if c == 0 else x_second[:, hf]
-
+        x_sb = [keep.tile([P, PACK, M], F32, name="x_sb%d" % c) for c in range(PASSES)]
         wd_raw = [keep.tile([P, T], F32, name="wd_raw%d" % i) for i in range(N_TILES)]
         x0_pass = [keep.tile([P, PACK, M], F32, name="x0_pass%d" % c) for c in range(PASSES)]
-        x0_sb = [x0_pass[i // PACK][:, i % PACK, :] for i in range(N_TILES - 2)]
-        x0_last = keep.tile([P, 2 * M], F32, name="x0_last", align_bytes=64)
-        x0_sb.extend((x0_last[:, :M], x0_last[:, M:]))
-        res_sb = [x0_pass[i // PACK][:, i % PACK, :] for i in range(N_TILES)]
-        ab_rows = keep.tile([P, K_PASS], F32, name="rows")
+        ab_rows = keep.tile([P, K_PASS], F32, name="ab_rows")
         g_row = keep.tile([P, K_PASS], F32, name="g_row")
-        ab_sb = keep.tile([P, 2 * PASSES, PACK], F32, name="columns")
-        g_sb = keep.tile([P, 1, PACK], F32, name="g_sb")
-        a_sb = [ab_sb[:, c, :] for c in range(PASSES)]
-        b_sb = [ab_sb[:, PASSES + c, :] for c in range(PASSES)]
+        ab_sb = keep.tile([P, 2, PASSES, PACK], F32, name="ab_sb")
+        g_sb = keep.tile([P, PACK], F32, name="g_sb")
         ident = keep.tile([P, P], F32, name="ident")
 
         nc.gpsimd.memset(tabs_raw[:].bitcast(I32), 0)
-        nc.vector.memset(w4s_raw[:].rearrange("p c n -> p (c n)").bitcast(I32), 0)
         nc.vector.memset(g_row[:], 0.0)
+        nc.vector.memset(w4s_raw[:].rearrange("p c n -> p (c n)").bitcast(I32), 0)
         nc.vector.memset(ab_rows[:], 0.0)
+        nc.gpsimd.memset(vs[:].rearrange("p c s -> p (c s)").bitcast(I32), 0)
         make_identity(nc, ident[:])
-        nc.gpsimd.memset(vs_words, 0)
 
         x_rows = x.rearrange("(c p t) m -> c p t m", p=P, t=PACK)
         x0_rows = x0.rearrange("(c p t) m -> c p t m", p=P, t=PACK)
         out_rows = out.rearrange("(c p t) m -> c p t m", p=P, t=PACK)
         wd_rows = wdT.rearrange("(c p t) j -> c t p j", p=P, t=PACK)
-
-        def load_x(c, hf):
-            nc.sync.dma_start(out=x_raw(c, hf), in_=x_rows[c][:, :, hf * HALF:(hf + 1) * HALF])
 
         def load_wd(i):
             nc.sync.dma_start(out=wd_raw[i][:], in_=wd_rows[i // PACK][i % PACK])
@@ -101,25 +92,20 @@ def tile_list_lowrank_cross_layer_kernel(
         def load_tab(c):
             nc.sync.dma_start(out=tab_raw[c][:], in_=tab_words[c].rearrange("p n t -> p (n t)").bitcast(I32))
 
-        def load_rows(tile, vector, row):
-            nc.sync.dma_start(out=tile[row:row + vector.shape[0] // K_PASS, :],
-                              in_=vector.rearrange("(c n) -> c n", n=K_PASS))
+        def load_w4_scales(rows):
+            for r in rows:
+                nc.sync.dma_start(out=w4s_raw[r:P:QUADRANT].bitcast(I32),
+                                  in_=w4_scales[:, r:16:LIVE, :].rearrange("c r n -> r c n").bitcast(I32))
 
-        def load_w4_scales(q):
-            nc.sync.dma_start(out=w4s_raw[q:P:QUADRANT].bitcast(I32),
-                              in_=w4_scales[:, q:16:LIVE, :].rearrange("c r n -> r c n").bitcast(I32))
-
-        nc.sync.dma_start(out=w4_raw[:].bitcast(I32), in_=w4_words.rearrange("c p n -> p c n").bitcast(I32))
+        load_tab(0)
         nc.sync.dma_start(offsets[:], offs)
         nc.sync.dma_start(out=tabs_raw[0:P:LIVE].bitcast(I32),
                           in_=tab_scales.rearrange("c z n -> z c n").bitcast(I32))
-        nc.sync.dma_start(out=x_first[:], in_=x_rows[0])
-        load_rows(g_row, g, ROW0)
-        for q in QUADRANTS[:-1]:
-            load_w4_scales(q)
-        load_tab(0)
+        nc.sync.dma_start(out=g_row[ROW0:ROW0 + 1, :], in_=g.rearrange("(c n) -> c n", c=1))
+        load_w4_scales((0, 1))
         load_tab(1)
-        load_w4_scales(QUADRANTS[-1])
+        nc.sync.dma_start(out=x_sb[0][:], in_=x_rows[0])
+        load_w4_scales((2, 3))
         vs_listed = keep.tile([P, S], U8, name="vs_listed", align_bytes=64)
         vs_dealt = keep.tile([P, S], U8, name="vs_dealt", align_bytes=64)
         nc.vector.tensor_copy(out=vs_listed[:], in_=tabs_raw[:].indirect(offsets[:]))
@@ -128,32 +114,26 @@ def tile_list_lowrank_cross_layer_kernel(
         for q in QUADRANTS:
             nc.sync.dma_start(out=vs[QUADRANT * q + LIVE:QUADRANT * q + 2 * LIVE].bitcast(I32),
                               in_=vs_dealt[QUADRANT * q:QUADRANT * (q + 1):LIVE].bitcast(I32))
-        load_x(1, 0)
-        load_x(1, 1)
-        load_rows(ab_rows, a, ROW0)
-        load_rows(ab_rows, b, ROW0 + PASSES)
-        for i in range(WD_AHEAD):
-            load_wd(i)
-        for i in range(N_TILES - 2):
-            load_wd(i + WD_AHEAD)
+        nc.sync.dma_start(out=x_sb[1][:], in_=x_rows[1])
+        for k, vector in enumerate((a, b)):
+            nc.sync.dma_start(out=ab_rows[ROW0 + LIVE * k:P:ROW_STEP, :],
+                              in_=vector.rearrange("(c n) -> c n", n=K_PASS))
+        nc.sync.dma_start(out=w4_raw[:].bitcast(I32), in_=w4_words.rearrange("c p n -> p c n").bitcast(I32))
+        load_wd(0)
+        load_wd(1)
+        for pair in range(X0_PAIRS):
+            load_x0(2 * pair, 2)
+            load_wd(2 * pair + 2)
+            load_wd(2 * pair + 3)
+        for i in range(2 * X0_PAIRS, N_TILES):
             load_x0(i, 1)
-        load_wd(N_TILES - 1)
-        nc.sync.dma_start(out=x0_last[:].rearrange("p (t m) -> p t m", t=2), in_=x0_rows[1][:, 2:4, :])
 
-        w4q = keep.tile([P, PASSES, 2 * N], U8, name="w4q", align_bytes=64)
-        w4s = keep.tile([P, PASSES, N], U8, name="w4s", align_bytes=64)
-        for c in range(PASSES):
-            nc.vector.tensor_copy(
-                out=w4q[:, c, :].bitcast(U16).rearrange("p (d t q) -> p d t q", t=PACK, q=P),
-                in_=w4_raw[:, c, :].bitcast(U16).rearrange("p (d q t) -> p d t q", t=PACK, q=P))
-
-        def turn_rows(dst, src, bank):
+        def turn_rows(src, bank):
             for t in range(PACK):
                 nc.tensor.transpose(bank[:, t * P:(t + 1) * P], src[:, t:K_PASS:PACK], ident[:])
-            nc.scalar.copy(out=dst[:],
-                           in_=bank[:].rearrange("p (t r) -> p r t", t=PACK)[:, ROW0:ROW0 + dst.shape[1], :])
+            return bank[:].rearrange("p (t r) -> p r t", t=PACK)
 
-        turn_rows(g_sb, g_row, h_banks[1][0])
+        nc.scalar.copy(out=g_sb[:], in_=turn_rows(g_row, banks[7])[:, ROW0, :])
 
         vq = [keep.tile([P, S], U32, name="vq%d" % c, align_bytes=64) for c in range(PASSES)]
         for c in range(PASSES):
@@ -167,25 +147,30 @@ def tile_list_lowrank_cross_layer_kernel(
                 xq[c, hf] = keep.tile([P, HALF], U32, name="xq%d%d" % (c, hf), align_bytes=64)
                 xs[c, hf] = keep.tile([P, HALF], U8, name="xs%d%d" % (c, hf), align_bytes=64)
 
-        low, high, whole = slice(0, HALF // 2), slice(HALF // 2, HALF), slice(0, HALF)
+        on_vector, on_scalar = nc.vector.tensor_copy, nc.scalar.copy
+        whole = slice(0, HALF)
+        both = ((on_vector, slice(0, VECTOR_SHARE)), (on_scalar, slice(VECTOR_SHARE, HALF)))
+        halves = ((on_vector, slice(0, HALF // 2)), (on_scalar, slice(HALF // 2, HALF)))
 
-        def weave(copy, woven, by_slot, cols):
-            copy(out=woven[:, cols.start * PACK:cols.stop * PACK].rearrange("p (m i t) -> p m t i", i=RUN, t=PACK),
-                 in_=by_slot[:, :, cols].rearrange("p t (m i) -> p m t i", i=RUN))
+        def columns(hf):
+            return slice(hf * HALF, (hf + 1) * HALF)
+
+        def weave(shares, woven, by_slot):
+            for copy, cols in shares:
+                copy(out=woven[:, cols.start * PACK:cols.stop * PACK].rearrange("p (m i t) -> p m t i", i=RUN, t=PACK),
+                     in_=by_slot[:, :, cols].rearrange("p t (m i) -> p m t i", i=RUN))
 
         def prepare_x(c, hf, shares):
             woven = ring.tile([P, HALF * PACK], BF16, name="woven", align_bytes=64, bufs=WOVEN_BUFS)
-            for copy, cols in shares:
-                weave(copy, woven, x_raw(c, hf), cols)
+            weave(shares, woven, x_sb[c][:, :, columns(hf)])
             nc.vector.quantize_mx(out=xq[c, hf][:].bitcast(FP8X4), scales=xs[c, hf][:], in_=woven[:])
             return woven
 
         hq = [keep.tile([P, HALF], U32, name="hq%d" % hf, align_bytes=64) for hf in range(HALVES)]
-        hs = [xs[1, 1][LIVE:, :], keep.tile([P, HALF], U8, name="hs1", align_bytes=64)[:]]
-        h_woven = {}
+        hs = [keep.tile([P, HALF], U8, name="hs%d" % hf, align_bytes=64) for hf in range(HALVES)]
 
-        def project(hf, shares, woven):
-            by_slot = ring.tile([P, PACK, HALF], BF16, name="h_planes")
+        def project(hf, vector_slots):
+            by_slot = ring.tile([P, PACK, HALF], BF16, name="h_by_slot")
             for t in range(PACK):
                 bank = h_banks[hf][t]
                 for c in range(PASSES):
@@ -193,16 +178,26 @@ def tile_list_lowrank_cross_layer_kernel(
                                         lhsT_scale=vs[LIVE:, c, t * P:(t + 1) * P],
                                         rhs=xq[c, hf][:].bitcast(FP8X4), rhs_scale=xs[c, hf][:],
                                         start=(c == 0), stop=(c == PASSES - 1))
-                nc.scalar.activation(out=by_slot[:, t, :], in_=bank[:], func=COPY, scale=g_sb[:, 0, t:t + 1])
-            for copy, cols in shares:
-                weave(copy, woven, by_slot, cols)
-            h_woven[hf] = woven
+                if t in vector_slots:
+                    nc.vector.tensor_scalar_mul(by_slot[:, t, :], bank[:], g_sb[:, t:t + 1])
+                else:
+                    nc.scalar.activation(out=by_slot[:, t, :], in_=bank[:], func=COPY, scale=g_sb[:, t:t + 1])
+            return by_slot
 
-        def quantise_h(hf, parts):
-            woven = h_woven[hf]
-            for cols in parts:
-                nc.vector.quantize_mx(out=hq[hf][:, cols].bitcast(FP8X4), scales=hs[hf][:, cols],
-                                      in_=woven[:, cols.start * PACK:cols.stop * PACK])
+        def quantise_h(hf, by_slot, shares, woven):
+            weave(shares, woven, by_slot)
+            nc.vector.quantize_mx(out=hq[hf][:].bitcast(FP8X4), scales=hs[hf][:], in_=woven[:])
+
+        w4s = keep.tile([P, PASSES, N], U8, name="w4s", align_bytes=64)
+
+
+        w4q = {}
+
+        def deal_w4_words(i):
+            d, t = i // PACK, i % PACK
+            w4q[i] = ring.tile([P, PASSES, 2 * P], U8, name="w4q", align_bytes=64, bufs=3)
+            nc.scalar.copy(out=w4q[i][:].bitcast(U16),
+                           in_=w4_raw[:].bitcast(U16)[:, :, d * K_PASS + t:(d + 1) * K_PASS:PACK])
 
         wdq = [keep.tile([P, P], U32, name="wdq%d" % i, align_bytes=64) for i in range(N_TILES)]
         wds = [keep.tile([P, P], U8, name="wds%d" % i, align_bytes=64) for i in range(N_TILES)]
@@ -214,13 +209,10 @@ def tile_list_lowrank_cross_layer_kernel(
 
         def turn_wd(i):
             pairs = wd_listed[i % 2][:].bitcast(F32)
-            bank = wd_banks[i % 2][:, :2 * P].rearrange("p (u n) -> p u n", u=2)
+            bank = wd_bank(i)[:, :2 * P].rearrange("p (u n) -> p u n", u=2)
             for u in range(2):
                 nc.tensor.transpose(bank[:, u, :], pairs[:, u:S // 2:2], ident[:])
-            if i < N_TILES - 1:
-                words = ring.tile([P, 2 * P], F32, name="wd_woven", align_bytes=64)[:]
-            else:
-                words = x0_sb[i - 1][:, :2 * P]
+            words = ring.tile([P, 2 * P], F32, name="wd_woven", align_bytes=64)[:]
             wd_woven[i] = words.bitcast(BF16)
             nc.scalar.copy(out=words.rearrange("p (n u) -> p n u", u=2), in_=bank.rearrange("p u n -> p n u"))
 
@@ -231,58 +223,59 @@ def tile_list_lowrank_cross_layer_kernel(
             c_out, t = i // PACK, i % PACK
             bank = y_bank(i, hf)
             for c in range(PASSES):
-                nc.tensor.matmul_mx(out=bank[:], lhsT=w4q[:, c, 2 * i * P:2 * (i + 1) * P].bitcast(FP4X4),
+                nc.tensor.matmul_mx(out=bank[:], lhsT=w4q[i][:, c, :].bitcast(FP4X4),
                                     lhsT_scale=w4s[:, c, i * P:(i + 1) * P],
                                     rhs=xq[c, hf][:].bitcast(FP8X4), rhs_scale=xs[c, hf][:],
                                     start=(c == 0), stop=False)
             nc.tensor.matmul_mx(out=bank[:], lhsT=wdq[i][:].bitcast(FP8X4), lhsT_scale=wds[i][:],
-                                rhs=hq[hf][:].bitcast(FP8X4), rhs_scale=hs[hf], start=False, stop=True)
-            cols = slice(hf * HALF, (hf + 1) * HALF)
-            nc.vector.scalar_tensor_tensor(out=res_sb[i][:, cols], in0=bank[:], scalar=b_sb[c_out][:, t:t + 1],
-                                           in1=x0_sb[i][:, cols], op0=ADD, op1=MULT)
+                                rhs=hq[hf][:].bitcast(FP8X4), rhs_scale=hs[hf][:], start=False, stop=True)
+            rows = x0_pass[c_out][:, t, columns(hf)]
+            nc.vector.scalar_tensor_tensor(out=rows, in0=bank[:], scalar=ab_sb[:, 1, c_out, t:t + 1],
+                                           in1=rows, op0=ADD, op1=MULT)
 
         def add_skip(i, hf):
             c_out, t = i // PACK, i % PACK
-            dst = res_sb[i][:, hf * HALF:(hf + 1) * HALF]
-            nc.vector.scalar_tensor_tensor(out=dst, in0=x_raw(c_out, hf)[:, t, :], scalar=a_sb[c_out][:, t:t + 1],
-                                           in1=dst, op0=MULT, op1=ADD)
+            rows = x0_pass[c_out][:, t, columns(hf)]
+            nc.vector.scalar_tensor_tensor(out=rows, in0=x_sb[c_out][:, t, columns(hf)],
+                                           scalar=ab_sb[:, 0, c_out, t:t + 1], in1=rows, op0=MULT, op1=ADD)
 
         def add_skip_beside(i):
             c_out, t = i // PACK, i % PACK
-            dst = res_sb[i][:, HALF:]
-            scaled = x_raw(c_out, 0)[:, t, :]
-            nc.scalar.activation(out=scaled, in_=x_raw(c_out, 1)[:, t, :], func=COPY, scale=a_sb[c_out][:, t:t + 1])
-            nc.gpsimd.tensor_tensor(out=dst, in0=dst, in1=scaled, op=ADD)
+            rows = x0_pass[c_out][:, t, columns(1)]
+            scaled = x_sb[c_out][:, t, columns(0)]
+            nc.scalar.activation(out=scaled, in_=x_sb[c_out][:, t, columns(1)], func=COPY,
+                                 scale=ab_sb[:, 0, c_out, t:t + 1])
+            nc.gpsimd.tensor_tensor(out=rows, in0=rows, in1=scaled, op=ADD)
 
         def store(first, count, cols):
             c_out, slots = first // PACK, slice(first % PACK, first % PACK + count)
             nc.sync.dma_start(out=out_rows[c_out][:, slots, cols], in_=x0_pass[c_out][:, slots, cols])
 
-        on_vector, on_scalar = nc.vector.tensor_copy, nc.scalar.copy
-        prepare_x(0, 0, ((on_scalar, whole),))
+        prepare_x(0, 0, ((on_vector, whole),))
         prepare_x(0, 1, ((on_scalar, whole),))
-        nc.vector.tensor_copy(
-            out=w4s[:].rearrange("p c (d t q) -> p (c d) t q", t=PACK, q=P),
-            in_=w4s_raw[:].rearrange("p c (d q t) -> p (c d) t q", t=PACK, q=P))
-        spent_first = prepare_x(1, 0, ((on_vector, low), (on_scalar, high)))
-        spent_last = prepare_x(1, 1, ((on_vector, whole),))
-        project(0, ((on_vector, whole),), spent_last)
-        project(1, ((on_vector, low), (on_scalar, high)), spent_first)
-        turn_rows(ab_sb, ab_rows, h_banks[0][0])
-        quantise_h(0, (whole,))
-        quantise_h(1, (low, high))
-        for i in range(WD_AHEAD):
-            gather_wd(i)
-            turn_wd(i)
-            quantise_wd(i)
+        nc.vector.tensor_copy(out=w4s[:].rearrange("p c (d t q) -> p (c d) t q", t=PACK, q=P),
+                              in_=w4s_raw[:].rearrange("p c (d q t) -> p (c d) t q", t=PACK, q=P))
+        spent_first = prepare_x(1, 0, both)
+        spent_last = prepare_x(1, 1, both)
+        h_first = project(0, (2, 3))
+        deal_w4_words(0)
+        h_second = project(1, ())
+        quantise_h(0, h_first, ((on_vector, whole),), spent_last)
+        gather_wd(0)
+        turn_wd(0)
+        ab_turned = turn_rows(ab_rows, banks[7]).rearrange("p (c r) t -> p r c t", c=PASSES)
+        nc.scalar.copy(out=ab_sb[:], in_=ab_turned[:, ROW0:ROW0 + 2 * LIVE:LIVE])
+        quantise_wd(0)
+        quantise_h(1, h_second, halves, spent_first)
 
         last = N_TILES - 1
         stores = {3: (0, 4), 5: (4, 2), 6: (6, 1)}
         beside = range(0, last - 1)
         for i in range(N_TILES):
-            ahead = i + WD_AHEAD
+            ahead = i + 1
             if ahead < N_TILES:
                 gather_wd(ahead)
+                deal_w4_words(ahead)
             cross(i, 0)
             cross(i, 1)
             if ahead < N_TILES:
@@ -291,7 +284,7 @@ def tile_list_lowrank_cross_layer_kernel(
                 quantise_wd(ahead)
             add_skip(i, 0)
             if i == last:
-                store(i, 1, slice(0, HALF))
+                store(i, 1, columns(0))
             if i not in beside:
                 add_skip(i, 1)
             if ahead < last:
@@ -300,4 +293,4 @@ def tile_list_lowrank_cross_layer_kernel(
                 add_skip_beside(i)
             if i in stores:
                 store(*stores[i], slice(0, M))
-        store(last, 1, slice(HALF, M))
+        store(last, 1, columns(1))

@@ -30,9 +30,9 @@ QUADRANT = 32
 LIVE = 4
 QUADRANTS = (0, 2, 1, 3)
 ROW0 = 16
+G_ROW = ROW0 + 2 * LIVE
 ROW_STEP = 64
 WOVEN_BUFS = 3
-X0_PAIRS = 3
 VECTOR_SHARE = 352
 
 
@@ -50,10 +50,7 @@ def tile_list_lowrank_cross_layer_kernel(
         def y_bank(i, hf):
             return banks[2 * (i % 3) + hf]
 
-        def wd_bank(i):
-            if i % 2 == 1 and i < 2 * X0_PAIRS:
-                return y_bank(i - 1, 0)
-            return banks[6]
+        ab_bank = banks[7]
 
         offsets = keep.tile([P, S // 16], U16, name="offsets")
         tabs_raw = keep.tile([P, T], U8, name="tabs_raw", align_bytes=64)
@@ -65,15 +62,13 @@ def tile_list_lowrank_cross_layer_kernel(
         wd_raw = [keep.tile([P, T], F32, name="wd_raw%d" % i) for i in range(N_TILES)]
         x0_pass = [keep.tile([P, PACK, M], F32, name="x0_pass%d" % c) for c in range(PASSES)]
         ab_rows = keep.tile([P, K_PASS], F32, name="ab_rows")
-        g_row = keep.tile([P, K_PASS], F32, name="g_row")
         ab_sb = keep.tile([P, 2, PASSES, PACK], F32, name="ab_sb")
         g_sb = keep.tile([P, PACK], F32, name="g_sb")
         ident = keep.tile([P, P], F32, name="ident")
 
         nc.gpsimd.memset(tabs_raw[:].bitcast(I32), 0)
-        nc.vector.memset(g_row[:], 0.0)
-        nc.vector.memset(w4s_raw[:].rearrange("p c n -> p (c n)").bitcast(I32), 0)
         nc.vector.memset(ab_rows[:], 0.0)
+        nc.vector.memset(w4s_raw[:].rearrange("p c n -> p (c n)").bitcast(I32), 0)
         nc.gpsimd.memset(vs[:].rearrange("p c s -> p (c s)").bitcast(I32), 0)
         make_identity(nc, ident[:])
 
@@ -101,11 +96,14 @@ def tile_list_lowrank_cross_layer_kernel(
         nc.sync.dma_start(offsets[:], offs)
         nc.sync.dma_start(out=tabs_raw[0:P:LIVE].bitcast(I32),
                           in_=tab_scales.rearrange("c z n -> z c n").bitcast(I32))
-        nc.sync.dma_start(out=g_row[ROW0:ROW0 + 1, :], in_=g.rearrange("(c n) -> c n", c=1))
-        load_w4_scales((0, 1))
-        load_tab(1)
+        nc.sync.dma_start(out=ab_rows[G_ROW:G_ROW + 1, :], in_=g.rearrange("(c n) -> c n", c=1))
+        for k, vector in enumerate((a, b)):
+            nc.sync.dma_start(out=ab_rows[ROW0 + LIVE * k:P:ROW_STEP, :],
+                              in_=vector.rearrange("(c n) -> c n", n=K_PASS))
+        load_w4_scales((0,))
         nc.sync.dma_start(out=x_sb[0][:], in_=x_rows[0])
-        load_w4_scales((2, 3))
+        load_w4_scales((1, 2, 3))
+        nc.sync.dma_start(out=x_sb[1][:], in_=x_rows[1])
         vs_listed = keep.tile([P, S], U8, name="vs_listed", align_bytes=64)
         vs_dealt = keep.tile([P, S], U8, name="vs_dealt", align_bytes=64)
         nc.vector.tensor_copy(out=vs_listed[:], in_=tabs_raw[:].indirect(offsets[:]))
@@ -114,29 +112,29 @@ def tile_list_lowrank_cross_layer_kernel(
         for q in QUADRANTS:
             nc.sync.dma_start(out=vs[QUADRANT * q + LIVE:QUADRANT * q + 2 * LIVE].bitcast(I32),
                               in_=vs_dealt[QUADRANT * q:QUADRANT * (q + 1):LIVE].bitcast(I32))
-        nc.sync.dma_start(out=x_sb[1][:], in_=x_rows[1])
-        for k, vector in enumerate((a, b)):
-            nc.sync.dma_start(out=ab_rows[ROW0 + LIVE * k:P:ROW_STEP, :],
-                              in_=vector.rearrange("(c n) -> c n", n=K_PASS))
+        load_tab(1)
         nc.sync.dma_start(out=w4_raw[:].bitcast(I32), in_=w4_words.rearrange("c p n -> p c n").bitcast(I32))
         load_wd(0)
         load_wd(1)
-        for pair in range(X0_PAIRS):
-            load_x0(2 * pair, 2)
-            load_wd(2 * pair + 2)
-            load_wd(2 * pair + 3)
-        for i in range(2 * X0_PAIRS, N_TILES):
-            load_x0(i, 1)
+        load_x0(0, 1)
+        for i in range(2, N_TILES):
+            load_wd(i)
+            load_x0(i - 1, 1)
+        load_x0(N_TILES - 1, 1)
 
         def turn_rows(src, bank):
             for t in range(PACK):
                 nc.tensor.transpose(bank[:, t * P:(t + 1) * P], src[:, t:K_PASS:PACK], ident[:])
             return bank[:].rearrange("p (t r) -> p r t", t=PACK)
 
-        nc.scalar.copy(out=g_sb[:], in_=turn_rows(g_row, banks[7])[:, ROW0, :])
+        turned = turn_rows(ab_rows, ab_bank)
+        nc.scalar.copy(out=g_sb[:], in_=turned[:, G_ROW, :])
+        ab_turned = turned.rearrange("p (c r) t -> p r c t", c=PASSES)
+        nc.scalar.copy(out=ab_sb[:], in_=ab_turned[:, ROW0:ROW0 + 2 * LIVE:LIVE])
 
         vq = [keep.tile([P, S], U32, name="vq%d" % c, align_bytes=64) for c in range(PASSES)]
-        for c in range(PASSES):
+
+        def gather_tab(c):
             nc.vector.tensor_copy(out=vq[c][:].rearrange("p (t q) -> p q t", t=PACK),
                                   in_=tab_raw[c][:].bitcast(U32).indirect(offsets[:]))
 
@@ -209,10 +207,10 @@ def tile_list_lowrank_cross_layer_kernel(
 
         def turn_wd(i):
             pairs = wd_listed[i % 2][:].bitcast(F32)
-            bank = wd_bank(i)[:, :2 * P].rearrange("p (u n) -> p u n", u=2)
+            bank = banks[6 + i % 2][:, :2 * P].rearrange("p (u n) -> p u n", u=2)
             for u in range(2):
                 nc.tensor.transpose(bank[:, u, :], pairs[:, u:S // 2:2], ident[:])
-            words = ring.tile([P, 2 * P], F32, name="wd_woven", align_bytes=64)[:]
+            words = ring.tile([P, 2 * P], F32, name="wd_woven", align_bytes=64, bufs=3)[:]
             wd_woven[i] = words.bitcast(BF16)
             nc.scalar.copy(out=words.rearrange("p (n u) -> p n u", u=2), in_=bank.rearrange("p u n -> p n u"))
 
@@ -251,20 +249,21 @@ def tile_list_lowrank_cross_layer_kernel(
             c_out, slots = first // PACK, slice(first % PACK, first % PACK + count)
             nc.sync.dma_start(out=out_rows[c_out][:, slots, cols], in_=x0_pass[c_out][:, slots, cols])
 
+        gather_tab(0)
         prepare_x(0, 0, ((on_vector, whole),))
         prepare_x(0, 1, ((on_scalar, whole),))
         nc.vector.tensor_copy(out=w4s[:].rearrange("p c (d t q) -> p (c d) t q", t=PACK, q=P),
                               in_=w4s_raw[:].rearrange("p c (d q t) -> p (c d) t q", t=PACK, q=P))
-        spent_first = prepare_x(1, 0, both)
-        spent_last = prepare_x(1, 1, both)
-        h_first = project(0, (2, 3))
+        spent_first = prepare_x(1, 0, ((on_vector, whole),))
+        spent_last = prepare_x(1, 1, ((on_scalar, whole),))
+        gather_tab(1)
         deal_w4_words(0)
+        deal_w4_words(1)
+        h_first = project(0, (2, 3))
         h_second = project(1, ())
         quantise_h(0, h_first, ((on_vector, whole),), spent_last)
         gather_wd(0)
         turn_wd(0)
-        ab_turned = turn_rows(ab_rows, banks[7]).rearrange("p (c r) t -> p r c t", c=PASSES)
-        nc.scalar.copy(out=ab_sb[:], in_=ab_turned[:, ROW0:ROW0 + 2 * LIVE:LIVE])
         quantise_wd(0)
         quantise_h(1, h_second, halves, spent_first)
 
@@ -275,6 +274,7 @@ def tile_list_lowrank_cross_layer_kernel(
             ahead = i + 1
             if ahead < N_TILES:
                 gather_wd(ahead)
+            if 1 < ahead < N_TILES:
                 deal_w4_words(ahead)
             cross(i, 0)
             cross(i, 1)

@@ -53,15 +53,15 @@ def tile_list_lowrank_cross_layer_kernel(
         ab_bank = banks[7]
 
         offsets = keep.tile([P, S // 16], U16, name="offsets")
-        tabs_raw = keep.tile([P, T], U8, name="tabs_raw", align_bytes=64)
-        tab_raw = [keep.tile([P, T], I32, name="tab_raw%d" % c, align_bytes=64) for c in range(PASSES)]
-        w4_raw = keep.tile([P, PASSES, 2 * N], U8, name="w4_raw", align_bytes=64)
-        w4s_raw = keep.tile([P, PASSES, N], U8, name="w4s_raw", align_bytes=64)
-        vs = keep.tile([P, PASSES, S], U8, name="vs", align_bytes=64)
-        x_sb = [keep.tile([P, PACK, M], F32, name="x_sb%d" % c) for c in range(PASSES)]
-        wd_raw = [keep.tile([P, T], F32, name="wd_raw%d" % i) for i in range(N_TILES)]
-        x0_pass = [keep.tile([P, PACK, M], F32, name="x0_pass%d" % c) for c in range(PASSES)]
-        ab_rows = keep.tile([P, K_PASS], F32, name="ab_rows")
+        tabs_raw = keep.tile([P, T], U8, name="tabs_raw", align_bytes=256)
+        tab_raw = [keep.tile([P, T], I32, name="tab_raw%d" % c, align_bytes=256) for c in range(PASSES)]
+        w4_raw = keep.tile([P, PASSES, 2 * N], U8, name="w4_raw", align_bytes=256)
+        w4s_raw = keep.tile([P, PASSES, N], U8, name="w4s_raw", align_bytes=256)
+        vs = keep.tile([P, PASSES, S], U8, name="vs", align_bytes=256)
+        x_sb = [keep.tile([P, PACK, M], F32, name="x_sb%d" % c, align_bytes=256) for c in range(PASSES)]
+        wd_raw = [keep.tile([P, T], F32, name="wd_raw%d" % i, align_bytes=256) for i in range(N_TILES)]
+        x0_pass = [keep.tile([P, PACK, M], F32, name="x0_pass%d" % c, align_bytes=256) for c in range(PASSES)]
+        ab_rows = keep.tile([P, K_PASS], F32, name="ab_rows", align_bytes=256)
         ab_sb = keep.tile([P, 2, PASSES, PACK], F32, name="ab_sb")
         g_sb = keep.tile([P, PACK], F32, name="g_sb")
         ident = keep.tile([P, P], F32, name="ident")
@@ -105,7 +105,7 @@ def tile_list_lowrank_cross_layer_kernel(
         load_w4_scales((1, 2, 3))
         nc.sync.dma_start(out=x_sb[1][:], in_=x_rows[1])
         vs_listed = keep.tile([P, S], U8, name="vs_listed", align_bytes=64)
-        vs_dealt = keep.tile([P, S], U8, name="vs_dealt", align_bytes=64)
+        vs_dealt = keep.tile([P, S], U8, name="vs_dealt", align_bytes=256)
         nc.vector.tensor_copy(out=vs_listed[:], in_=tabs_raw[:].indirect(offsets[:]))
         nc.vector.tensor_copy(out=vs_dealt[:].rearrange("p (t q) -> p t q", t=PACK),
                               in_=vs_listed[:].rearrange("p (q t) -> p t q", t=PACK))

@@ -259,9 +259,20 @@ def tile_list_lowrank_cross_layer_kernel(
         gather_tab(1)
         deal_w4_words(0)
         deal_w4_words(1)
-        h_first = project(0, (2, 3))
+        for c in range(PASSES):
+            for u, bank in enumerate(h_banks[0]):
+                cols = slice(u * P, (u + 1) * P)
+                for t in range(PACK):
+                    nc.tensor.matmul_mx(out=bank[:, t * P:(t + 1) * P], lhsT=vq[c][:, t * P:(t + 1) * P].bitcast(FP8X4),
+                                        lhsT_scale=vs[LIVE:, c, t * P:(t + 1) * P],
+                                        rhs=xq[c, 0][:, cols].bitcast(FP8X4), rhs_scale=xs[c, 0][:, cols],
+                                        start=(c == 0 and t == 0), stop=(c == PASSES - 1 and t == PACK - 1))
         h_second = project(1, ())
-        quantise_h(0, h_first, ((on_vector, whole),), spent_last)
+        gains = g_sb[:].unsqueeze(1).to_broadcast([P, P, PACK])
+        for u, bank in enumerate(h_banks[0]):
+            nc.vector.tensor_tensor(out=spent_last[:, u * K_PASS:(u + 1) * K_PASS].rearrange("p (m t) -> p m t", t=PACK),
+                                    in0=bank[:].rearrange("p (t m) -> p m t", t=PACK), in1=gains, op=MULT)
+        nc.vector.quantize_mx(out=hq[0][:].bitcast(FP8X4), scales=hs[0][:], in_=spent_last[:])
         gather_wd(0)
         turn_wd(0)
         quantise_wd(0)

@@ -54,7 +54,8 @@ def tile_list_lowrank_cross_layer_kernel(
 
         offsets = keep.tile([P, S // 16], U16, name="offsets")
         tabs_raw = keep.tile([P, T], U8, name="tabs_raw", align_bytes=256)
-        tab_raw = [keep.tile([P, T], I32, name="tab_raw%d" % c, align_bytes=256) for c in range(PASSES)]
+        tab_raw = [keep.tile([P, T], I32, name="tab_raw%d" % c, tag="tab_raw%d" % c, align_bytes=256)
+                   for c in range(PASSES)]
         w4_raw = keep.tile([P, PASSES, 2 * N], U8, name="w4_raw", align_bytes=256)
         w4s_raw = keep.tile([P, PASSES, N], U8, name="w4s_raw", align_bytes=256)
         vs = keep.tile([P, PASSES, S], U8, name="vs", align_bytes=256)
@@ -142,7 +143,8 @@ def tile_list_lowrank_cross_layer_kernel(
         xs = {}
         for c in range(PASSES):
             for hf in range(HALVES):
-                xq[c, hf] = keep.tile([P, HALF], U32, name="xq%d%d" % (c, hf), align_bytes=64)
+                if (c, hf) != (PASSES - 1, HALVES - 1):
+                    xq[c, hf] = keep.tile([P, HALF], U32, name="xq%d%d" % (c, hf), align_bytes=64)
                 xs[c, hf] = keep.tile([P, HALF], U8, name="xs%d%d" % (c, hf), align_bytes=64)
 
         on_vector, on_scalar = nc.vector.tensor_copy, nc.scalar.copy
@@ -167,20 +169,11 @@ def tile_list_lowrank_cross_layer_kernel(
         hq = [keep.tile([P, HALF], U32, name="hq%d" % hf, align_bytes=64) for hf in range(HALVES)]
         hs = [keep.tile([P, HALF], U8, name="hs%d" % hf, align_bytes=64) for hf in range(HALVES)]
 
-        def project(hf, vector_slots):
-            by_slot = ring.tile([P, PACK, HALF], BF16, name="h_by_slot")
-            for t in range(PACK):
-                bank = h_banks[hf][t]
-                for c in range(PASSES):
-                    nc.tensor.matmul_mx(out=bank[:], lhsT=vq[c][:, t * P:(t + 1) * P].bitcast(FP8X4),
-                                        lhsT_scale=vs[LIVE:, c, t * P:(t + 1) * P],
-                                        rhs=xq[c, hf][:].bitcast(FP8X4), rhs_scale=xs[c, hf][:],
-                                        start=(c == 0), stop=(c == PASSES - 1))
-                if t in vector_slots:
-                    nc.vector.tensor_scalar_mul(by_slot[:, t, :], bank[:], g_sb[:, t:t + 1])
-                else:
-                    nc.scalar.activation(out=by_slot[:, t, :], in_=bank[:], func=COPY, scale=g_sb[:, t:t + 1])
-            return by_slot
+        def project_pass(c, t, hf, cols, dest, start, stop):
+            nc.tensor.matmul_mx(out=dest, lhsT=vq[c][:, t * P:(t + 1) * P].bitcast(FP8X4),
+                                lhsT_scale=vs[LIVE:, c, t * P:(t + 1) * P],
+                                rhs=xq[c, hf][:, cols].bitcast(FP8X4), rhs_scale=xs[c, hf][:, cols],
+                                start=start, stop=stop)
 
         def quantise_h(hf, by_slot, shares, woven):
             weave(shares, woven, by_slot)
@@ -255,19 +248,21 @@ def tile_list_lowrank_cross_layer_kernel(
         nc.vector.tensor_copy(out=w4s[:].rearrange("p c (d t q) -> p (c d) t q", t=PACK, q=P),
                               in_=w4s_raw[:].rearrange("p c (d q t) -> p (c d) t q", t=PACK, q=P))
         spent_first = prepare_x(1, 0, ((on_vector, whole),))
-        spent_last = prepare_x(1, 1, ((on_scalar, whole),))
         gather_tab(1)
+        xq[1, 1] = keep.tile([P, HALF], U32, name="xq11", tag="tab_raw1", align_bytes=256)
+        spent_last = prepare_x(1, 1, ((on_scalar, whole),))
         deal_w4_words(0)
         deal_w4_words(1)
         for c in range(PASSES):
             for u, bank in enumerate(h_banks[0]):
-                cols = slice(u * P, (u + 1) * P)
                 for t in range(PACK):
-                    nc.tensor.matmul_mx(out=bank[:, t * P:(t + 1) * P], lhsT=vq[c][:, t * P:(t + 1) * P].bitcast(FP8X4),
-                                        lhsT_scale=vs[LIVE:, c, t * P:(t + 1) * P],
-                                        rhs=xq[c, 0][:, cols].bitcast(FP8X4), rhs_scale=xs[c, 0][:, cols],
-                                        start=(c == 0 and t == 0), stop=(c == PASSES - 1 and t == PACK - 1))
-        h_second = project(1, ())
+                    project_pass(c, t, 0, slice(u * P, (u + 1) * P), bank[:, t * P:(t + 1) * P],
+                                 c == 0 and t == 0, c == PASSES - 1 and t == PACK - 1)
+            for t, bank in enumerate(h_banks[1]):
+                project_pass(c, t, 1, whole, bank[:], c == 0, c == PASSES - 1)
+        h_second = keep.tile([P, PACK, HALF], BF16, name="h_by_slot")
+        for t, bank in enumerate(h_banks[1]):
+            nc.scalar.activation(out=h_second[:, t, :], in_=bank[:], func=COPY, scale=g_sb[:, t:t + 1])
         gains = g_sb[:].unsqueeze(1).to_broadcast([P, P, PACK])
         for u, bank in enumerate(h_banks[0]):
             nc.vector.tensor_tensor(out=spent_last[:, u * K_PASS:(u + 1) * K_PASS].rearrange("p (m t) -> p m t", t=PACK),

@@ -238,9 +238,11 @@ def tile_list_lowrank_cross_layer_kernel(
                                  scale=ab_sb[:, 0, c_out, t:t + 1])
             nc.gpsimd.tensor_tensor(out=rows, in0=rows, in1=scaled, op=ADD)
 
-        def store(first, count, cols):
-            c_out, slots = first // PACK, slice(first % PACK, first % PACK + count)
-            nc.sync.dma_start(out=out_rows[c_out][:, slots, cols], in_=x0_pass[c_out][:, slots, cols])
+        def store(first, count):
+            c_out, start = divmod(first * HALF, PACK * M)
+            run = slice(start, start + count * HALF)
+            nc.sync.dma_start(out=out_rows[c_out].rearrange("p t m -> p (t m)")[:, run],
+                              in_=x0_pass[c_out][:].rearrange("p t m -> p (t m)")[:, run])
 
         gather_tab(0)
         prepare_x(0, 0, ((on_vector, whole),))
@@ -274,7 +276,7 @@ def tile_list_lowrank_cross_layer_kernel(
         quantise_h(1, h_second, halves, spent_first)
 
         last = N_TILES - 1
-        stores = {3: (0, 4), 5: (4, 2), 6: (6, 1)}
+        stores = {3: (0, 8), 5: (8, 3), 6: (11, 3)}
         beside = range(0, last - 1)
         for i in range(N_TILES):
             ahead = i + 1
@@ -290,7 +292,7 @@ def tile_list_lowrank_cross_layer_kernel(
                 quantise_wd(ahead)
             add_skip(i, 0)
             if i == last:
-                store(i, 1, columns(0))
+                store(HALVES * i, 1)
             if i not in beside:
                 add_skip(i, 1)
             if ahead < last:
@@ -298,5 +300,5 @@ def tile_list_lowrank_cross_layer_kernel(
             if i in beside:
                 add_skip_beside(i)
             if i in stores:
-                store(*stores[i], slice(0, M))
-        store(last, 1, columns(1))
+                store(*stores[i])
+        store(HALVES * last + 1, 1)

@@ -238,10 +238,10 @@ def tile_list_lowrank_cross_layer_kernel(
                                  scale=ab_sb[:, 0, c_out, t:t + 1])
             nc.gpsimd.tensor_tensor(out=rows, in0=rows, in1=scaled, op=ADD)
 
-        def store(first, count):
+        def store(first, count, queue):
             c_out, start = divmod(first * HALF, PACK * M)
             run = slice(start, start + count * HALF)
-            nc.sync.dma_start(out=out_rows[c_out].rearrange("p t m -> p (t m)")[:, run],
+            queue.dma_start(out=out_rows[c_out].rearrange("p t m -> p (t m)")[:, run],
                               in_=x0_pass[c_out][:].rearrange("p t m -> p (t m)")[:, run])
 
         gather_tab(0)
@@ -276,7 +276,7 @@ def tile_list_lowrank_cross_layer_kernel(
         quantise_h(1, h_second, halves, spent_first)
 
         last = N_TILES - 1
-        stores = {3: (0, 8), 5: (8, 3), 6: (11, 3)}
+        stores = {3: (0, 8, nc.sync), 5: (8, 3, nc.scalar), 6: (11, 3, nc.sync)}
         beside = range(0, last - 1)
         for i in range(N_TILES):
             ahead = i + 1
@@ -292,7 +292,7 @@ def tile_list_lowrank_cross_layer_kernel(
                 quantise_wd(ahead)
             add_skip(i, 0)
             if i == last:
-                store(HALVES * i, 1)
+                store(HALVES * i, 1, nc.scalar)
             if i not in beside:
                 add_skip(i, 1)
             if ahead < last:
@@ -301,4 +301,4 @@ def tile_list_lowrank_cross_layer_kernel(
                 add_skip_beside(i)
             if i in stores:
                 store(*stores[i])
-        store(HALVES * last + 1, 1)
+        store(HALVES * last + 1, 1, nc.sync)

from contextlib import ExitStack

import concourse.mybir as mybir
from concourse.masks import make_identity

K, N, T, S, M = 1024, 1024, 2048, 512, 1024
FLOPS = 2 * M * (K * S + K * N + S * N)

F32 = mybir.dt.float32
BF16 = mybir.dt.bfloat16
I32 = mybir.dt.int32
U32 = mybir.dt.uint32
U16 = mybir.dt.uint16
U8 = mybir.dt.uint8
FP8X4 = mybir.dt.float8_e4m3fn_x4
FP4X4 = mybir.dt.float4_e2m1fn_x4
MULT = mybir.AluOpType.mult
ADD = mybir.AluOpType.add
COPY = mybir.ActivationFunctionType.Copy

P = 128
PACK = 4
K_PASS = P * PACK
PASSES = K // K_PASS
HALF = 512
HALVES = M // HALF
N_TILES = N // P
RUN = 4
QUADRANT = 32
LIVE = 4
QUADRANTS = (0, 2, 1, 3)
ROW0 = 16
G_ROW = ROW0 + 2 * LIVE
ROW_STEP = 64
WOVEN_BUFS = 3
VECTOR_SHARE = 352


def tile_list_lowrank_cross_layer_kernel(
    tc, x, x0, tab_words, tab_scales, offs, g, wdT, w4_words, w4_scales, b, a, out
):
    nc = tc.nc
    with ExitStack() as ctx:
        keep = ctx.enter_context(tc.tile_pool(name="keep", bufs=1))
        ring = ctx.enter_context(tc.tile_pool(name="ring", bufs=2))
        psum = ctx.enter_context(tc.psum_pool(name="psum", bufs=1))
        banks = [psum.tile([P, HALF], F32, name="bank%d" % k) for k in range(8)]
        h_banks = (banks[:2] + banks[6:], banks[2:6])

        def y_bank(i, hf):
            return banks[2 * (i % 3) + hf]

        ab_bank = banks[7]

        offsets = keep.tile([P, S // 16], U16, name="offsets")
        tabs_raw = keep.tile([P, T], U8, name="tabs_raw", align_bytes=256)
        tab_raw = [keep.tile([P, T], I32, name="tab_raw%d" % c, tag="tab_raw%d" % c, align_bytes=256)
                   for c in range(PASSES)]
        w4_raw = keep.tile([P, PASSES, 2 * N], U8, name="w4_raw", align_bytes=256)
        w4s_raw = keep.tile([P, PASSES, N], U8, name="w4s_raw", align_bytes=256)
        vs = keep.tile([P, PASSES, S], U8, name="vs", align_bytes=256)
        x_sb = [keep.tile([P, PACK, M], F32, name="x_sb%d" % c, align_bytes=256) for c in range(PASSES)]
        wd_raw = [keep.tile([P, T], F32, name="wd_raw%d" % i, align_bytes=256) for i in range(N_TILES)]
        x0_pass = [keep.tile([P, PACK, M], F32, name="x0_pass%d" % c, align_bytes=256) for c in range(PASSES)]
        ab_rows = keep.tile([P, K_PASS], F32, name="ab_rows", align_bytes=256)
        ab_sb = keep.tile([P, 2, PASSES, PACK], F32, name="ab_sb")
        g_sb = keep.tile([P, PACK], F32, name="g_sb")
        ident = keep.tile([P, P], F32, name="ident")

        nc.gpsimd.memset(tabs_raw[:].bitcast(I32), 0)
        nc.vector.memset(ab_rows[:], 0.0)
        nc.vector.memset(w4s_raw[:].rearrange("p c n -> p (c n)").bitcast(I32), 0)
        nc.gpsimd.memset(vs[:].rearrange("p c s -> p (c s)").bitcast(I32), 0)
        make_identity(nc, ident[:])

        x_rows = x.rearrange("(c p t) m -> c p t m", p=P, t=PACK)
        x0_rows = x0.rearrange("(c p t) m -> c p t m", p=P, t=PACK)
        out_rows = out.rearrange("(c p t) m -> c p t m", p=P, t=PACK)
        wd_rows = wdT.rearrange("(c p t) j -> c t p j", p=P, t=PACK)

        def load_wd(i):
            nc.sync.dma_start(out=wd_raw[i][:], in_=wd_rows[i // PACK][i % PACK])

        def load_x0(first, count):
            slots = slice(first % PACK, first % PACK + count)
            nc.sync.dma_start(out=x0_pass[first // PACK][:, slots, :], in_=x0_rows[first // PACK][:, slots, :])

        def load_tab(c):
            nc.sync.dma_start(out=tab_raw[c][:], in_=tab_words[c].rearrange("p n t -> p (n t)").bitcast(I32))

        def load_w4_scales(rows):
            for r in rows:
                nc.sync.dma_start(out=w4s_raw[r:P:QUADRANT].bitcast(I32),
                                  in_=w4_scales[:, r:16:LIVE, :].rearrange("c r n -> r c n").bitcast(I32))

        load_tab(0)
        nc.sync.dma_start(offsets[:], offs)
        nc.sync.dma_start(out=tabs_raw[0:P:LIVE].bitcast(I32),
                          in_=tab_scales.rearrange("c z n -> z c n").bitcast(I32))
        nc.sync.dma_start(out=ab_rows[G_ROW:G_ROW + 1, :], in_=g.rearrange("(c n) -> c n", c=1))
        for k, vector in enumerate((a, b)):
            nc.sync.dma_start(out=ab_rows[ROW0 + LIVE * k:P:ROW_STEP, :],
                              in_=vector.rearrange("(c n) -> c n", n=K_PASS))
        load_w4_scales((0,))
        nc.sync.dma_start(out=x_sb[0][:], in_=x_rows[0])
        load_w4_scales((1, 2, 3))
        nc.sync.dma_start(out=x_sb[1][:], in_=x_rows[1])
        vs_listed = keep.tile([P, S], U8, name="vs_listed", align_bytes=64)
        vs_dealt = keep.tile([P, S], U8, name="vs_dealt", align_bytes=256)
        nc.vector.tensor_copy(out=vs_listed[:], in_=tabs_raw[:].indirect(offsets[:]))
        nc.vector.tensor_copy(out=vs_dealt[:].rearrange("p (t q) -> p t q", t=PACK),
                              in_=vs_listed[:].rearrange("p (q t) -> p t q", t=PACK))
        for q in QUADRANTS:
            nc.sync.dma_start(out=vs[QUADRANT * q + LIVE:QUADRANT * q + 2 * LIVE].bitcast(I32),
                              in_=vs_dealt[QUADRANT * q:QUADRANT * (q + 1):LIVE].bitcast(I32))
        load_tab(1)
        nc.sync.dma_start(out=w4_raw[:].bitcast(I32), in_=w4_words.rearrange("c p n -> p c n").bitcast(I32))
        load_wd(0)
        load_wd(1)
        load_x0(0, 1)
        for i in range(2, N_TILES):
            load_wd(i)
            load_x0(i - 1, 1)
        load_x0(N_TILES - 1, 1)

        def turn_rows(src, bank):
            for t in range(PACK):
                nc.tensor.transpose(bank[:, t * P:(t + 1) * P], src[:, t:K_PASS:PACK], ident[:])
            return bank[:].rearrange("p (t r) -> p r t", t=PACK)

        turned = turn_rows(ab_rows, ab_bank)
        nc.scalar.copy(out=g_sb[:], in_=turned[:, G_ROW, :])
        ab_turned = turned.rearrange("p (c r) t -> p r c t", c=PASSES)
        nc.scalar.copy(out=ab_sb[:], in_=ab_turned[:, ROW0:ROW0 + 2 * LIVE:LIVE])

        vq = [keep.tile([P, S], U32, name="vq%d" % c, align_bytes=64) for c in range(PASSES)]

        def gather_tab(c):
            nc.vector.tensor_copy(out=vq[c][:].rearrange("p (t q) -> p q t", t=PACK),
                                  in_=tab_raw[c][:].bitcast(U32).indirect(offsets[:]))

        xq = {}
        xs = {}
        for c in range(PASSES):
            for hf in range(HALVES):
                if (c, hf) != (PASSES - 1, HALVES - 1):
                    xq[c, hf] = keep.tile([P, HALF], U32, name="xq%d%d" % (c, hf), align_bytes=64)
                xs[c, hf] = keep.tile([P, HALF], U8, name="xs%d%d" % (c, hf), align_bytes=64)

        on_vector, on_scalar = nc.vector.tensor_copy, nc.scalar.copy
        whole = slice(0, HALF)
        both = ((on_vector, slice(0, VECTOR_SHARE)), (on_scalar, slice(VECTOR_SHARE, HALF)))
        halves = ((on_vector, slice(0, HALF // 2)), (on_scalar, slice(HALF // 2, HALF)))

        def columns(hf):
            return slice(hf * HALF, (hf + 1) * HALF)

        def weave(shares, woven, by_slot):
            for copy, cols in shares:
                copy(out=woven[:, cols.start * PACK:cols.stop * PACK].rearrange("p (m i t) -> p m t i", i=RUN, t=PACK),
                     in_=by_slot[:, :, cols].rearrange("p t (m i) -> p m t i", i=RUN))

        def prepare_x(c, hf, shares):
            woven = ring.tile([P, HALF * PACK], BF16, name="woven", align_bytes=64, bufs=WOVEN_BUFS)
            weave(shares, woven, x_sb[c][:, :, columns(hf)])
            nc.vector.quantize_mx(out=xq[c, hf][:].bitcast(FP8X4), scales=xs[c, hf][:], in_=woven[:])
            return woven

        hq = [keep.tile([P, HALF], U32, name="hq%d" % hf, align_bytes=64) for hf in range(HALVES)]
        hs = [keep.tile([P, HALF], U8, name="hs%d" % hf, align_bytes=64) for hf in range(HALVES)]

        def project_pass(c, t, hf, cols, dest, start, stop):
            nc.tensor.matmul_mx(out=dest, lhsT=vq[c][:, t * P:(t + 1) * P].bitcast(FP8X4),
                                lhsT_scale=vs[LIVE:, c, t * P:(t + 1) * P],
                                rhs=xq[c, hf][:, cols].bitcast(FP8X4), rhs_scale=xs[c, hf][:, cols],
                                start=start, stop=stop)

        def quantise_h(hf, by_slot, shares, woven):
            weave(shares, woven, by_slot)
            nc.vector.quantize_mx(out=hq[hf][:].bitcast(FP8X4), scales=hs[hf][:], in_=woven[:])

        w4s = keep.tile([P, PASSES, N], U8, name="w4s", align_bytes=64)


        w4q = {}

        def deal_w4_words(i):
            d, t = i // PACK, i % PACK
            w4q[i] = ring.tile([P, PASSES, 2 * P], U8, name="w4q", align_bytes=64, bufs=3)
            nc.scalar.copy(out=w4q[i][:].bitcast(U16),
                           in_=w4_raw[:].bitcast(U16)[:, :, d * K_PASS + t:(d + 1) * K_PASS:PACK])

        wdq = [keep.tile([P, P], U32, name="wdq%d" % i, align_bytes=64) for i in range(N_TILES)]
        wds = [keep.tile([P, P], U8, name="wds%d" % i, align_bytes=64) for i in range(N_TILES)]
        wd_woven = {}
        wd_listed = [keep.tile([P, S], BF16, name="wd_listed%d" % r, align_bytes=64) for r in range(2)]

        def gather_wd(i):
            nc.vector.tensor_copy(out=wd_listed[i % 2][:], in_=wd_raw[i][:].indirect(offsets[:]))

        def turn_wd(i):
            pairs = wd_listed[i % 2][:].bitcast(F32)
            bank = banks[6 + i % 2][:, :2 * P].rearrange("p (u n) -> p u n", u=2)
            for u in range(2):
                nc.tensor.transpose(bank[:, u, :], pairs[:, u:S // 2:2], ident[:])
            words = ring.tile([P, 2 * P], F32, name="wd_woven", align_bytes=64, bufs=3)[:]
            wd_woven[i] = words.bitcast(BF16)
            nc.scalar.copy(out=words.rearrange("p (n u) -> p n u", u=2), in_=bank.rearrange("p u n -> p n u"))

        def quantise_wd(i):
            nc.vector.quantize_mx(out=wdq[i][:].bitcast(FP8X4), scales=wds[i][:], in_=wd_woven[i])

        def cross(i, hf):
            c_out, t = i // PACK, i % PACK
            bank = y_bank(i, hf)
            for c in range(PASSES):
                nc.tensor.matmul_mx(out=bank[:], lhsT=w4q[i][:, c, :].bitcast(FP4X4),
                                    lhsT_scale=w4s[:, c, i * P:(i + 1) * P],
                                    rhs=xq[c, hf][:].bitcast(FP8X4), rhs_scale=xs[c, hf][:],
                                    start=(c == 0), stop=False)
            nc.tensor.matmul_mx(out=bank[:], lhsT=wdq[i][:].bitcast(FP8X4), lhsT_scale=wds[i][:],
                                rhs=hq[hf][:].bitcast(FP8X4), rhs_scale=hs[hf][:], start=False, stop=True)
            rows = x0_pass[c_out][:, t, columns(hf)]
            nc.vector.scalar_tensor_tensor(out=rows, in0=bank[:], scalar=ab_sb[:, 1, c_out, t:t + 1],
                                           in1=rows, op0=ADD, op1=MULT)

        def add_skip(i, hf):
            c_out, t = i // PACK, i % PACK
            rows = x0_pass[c_out][:, t, columns(hf)]
            nc.vector.scalar_tensor_tensor(out=rows, in0=x_sb[c_out][:, t, columns(hf)],
                                           scalar=ab_sb[:, 0, c_out, t:t + 1], in1=rows, op0=MULT, op1=ADD)

        def add_skip_beside(i):
            c_out, t = i // PACK, i % PACK
            rows = x0_pass[c_out][:, t, columns(1)]
            scaled = x_sb[c_out][:, t, columns(0)]
            nc.scalar.activation(out=scaled, in_=x_sb[c_out][:, t, columns(1)], func=COPY,
                                 scale=ab_sb[:, 0, c_out, t:t + 1])
            nc.gpsimd.tensor_tensor(out=rows, in0=rows, in1=scaled, op=ADD)

        def store(first, count, queue):
            c_out, start = divmod(first * HALF, PACK * M)
            run = slice(start, start + count * HALF)
            queue.dma_start(out=out_rows[c_out].rearrange("p t m -> p (t m)")[:, run],
                              in_=x0_pass[c_out][:].rearrange("p t m -> p (t m)")[:, run])

        gather_tab(0)
        prepare_x(0, 0, ((on_vector, whole),))
        prepare_x(0, 1, ((on_scalar, whole),))
        nc.vector.tensor_copy(out=w4s[:].rearrange("p c (d t q) -> p (c d) t q", t=PACK, q=P),
                              in_=w4s_raw[:].rearrange("p c (d q t) -> p (c d) t q", t=PACK, q=P))
        spent_first = prepare_x(1, 0, ((on_vector, whole),))
        gather_tab(1)
        xq[1, 1] = keep.tile([P, HALF], U32, name="xq11", tag="tab_raw1", align_bytes=256)
        spent_last = prepare_x(1, 1, ((on_scalar, whole),))
        deal_w4_words(0)
        deal_w4_words(1)
        for c in range(PASSES):
            for u, bank in enumerate(h_banks[0]):
                for t in range(PACK):
                    project_pass(c, t, 0, slice(u * P, (u + 1) * P), bank[:, t * P:(t + 1) * P],
                                 c == 0 and t == 0, c == PASSES - 1 and t == PACK - 1)
            for t, bank in enumerate(h_banks[1]):
                project_pass(c, t, 1, whole, bank[:], c == 0, c == PASSES - 1)
        h_second = keep.tile([P, PACK, HALF], BF16, name="h_by_slot")
        for t, bank in enumerate(h_banks[1]):
            nc.scalar.activation(out=h_second[:, t, :], in_=bank[:], func=COPY, scale=g_sb[:, t:t + 1])
        gains = g_sb[:].unsqueeze(1).to_broadcast([P, P, PACK])
        for u, bank in enumerate(h_banks[0]):
            nc.vector.tensor_tensor(out=spent_last[:, u * K_PASS:(u + 1) * K_PASS].rearrange("p (m t) -> p m t", t=PACK),
                                    in0=bank[:].rearrange("p (t m) -> p m t", t=PACK), in1=gains, op=MULT)
        nc.vector.quantize_mx(out=hq[0][:].bitcast(FP8X4), scales=hs[0][:], in_=spent_last[:])
        gather_wd(0)
        turn_wd(0)
        quantise_wd(0)
        quantise_h(1, h_second, halves, spent_first)

        last = N_TILES - 1
        stores = {3: (0, 8, nc.sync), 5: (8, 3, nc.scalar), 6: (11, 3, nc.sync)}
        beside = range(0, last - 1)
        for i in range(N_TILES):
            ahead = i + 1
            if ahead < N_TILES:
                gather_wd(ahead)
            if 1 < ahead < N_TILES:
                deal_w4_words(ahead)
            cross(i, 0)
            cross(i, 1)
            if ahead < N_TILES:
                turn_wd(ahead)
            if ahead == last:
                quantise_wd(ahead)
            add_skip(i, 0)
            if i == last:
                store(HALVES * i, 1, nc.scalar)
            if i not in beside:
                add_skip(i, 1)
            if ahead < last:
                quantise_wd(ahead)
            if i in beside:
                add_skip_beside(i)
            if i in stores:
                store(*stores[i])
        store(HALVES * last + 1, 1, nc.sync)
